import numpy as np, ml_dtypes
CORES = [9,25,41,57]
N = 4
import mx_ref
BF = ml_dtypes.bfloat16
def gcols(t, e):
    v = np.concatenate([t.reshape(8, 16, -1, 4), np.zeros((8, 16, 1, 4), BF)], axis=2)
    return np.ascontiguousarray(np.stack([v[g][:, e[g]] for g in range(8)])).reshape(128, -1)
def tile(rs):
    return np.stack(rs, axis=2).reshape(128, -1).astype(BF)
def cut(t, i, w=512):
    return t[:, w * i:w * i + w]
def gentries(a):
    return np.ascontiguousarray(a.reshape(8, 16, -1).transpose(0, 2, 1)).reshape(8, -1)
def gtable(e):
    e = np.asarray(e); return np.ascontiguousarray(e.reshape(8, -1, 16).transpose(0, 2, 1)).reshape(128, -1).astype(np.int32)
def pick(q, e):
    c = np.concatenate([q[0].reshape(128, -1, 4), np.zeros((128, 1, 4), np.uint8)], axis=1); s = np.concatenate([q[1], np.ones((16, 1), np.uint8)], axis=1)
    return (np.ascontiguousarray(c[:, e].reshape(128, -1)), np.ascontiguousarray(s[:, e]))
def join(*qs):
    return (np.concatenate([q[0] for q in qs], axis=1), np.concatenate([q[1] for q in qs], axis=1))
def put(q, e, v):
    c, s = q[0].reshape(128, -1, 4).copy(), q[1].copy(); c[:, e] = v[0].reshape(128, -1, 4); s[:, e] = v[1]
    return (c.reshape(128, -1), s)
def pk(c, s):
    return (np.ascontiguousarray(c), mx_ref.live(s))
def emit(q):
    return q[0], q[1]
def packed(v, rng):
    q = [mx_ref.quantize(np.ascontiguousarray(v[r])) for r in range(N)]
    return np.stack([a for a, b in q]), np.stack([mx_ref.plane(b, rng) for a, b in q])
def values_of_codes():
    e, c = np.zeros((128, 128, 4), np.float32), np.zeros((128, 2, 4), np.uint8)
    e[np.arange(128), np.arange(128), 0] = 1
    c[:127, :, 0] = np.arange(256).reshape(2, 128).T[:127]
    return mx_ref.matmul(mx_ref.quantize(e.reshape(128, 512).astype(BF)), (c.reshape(128, 8), np.full((16, 2), 127, np.uint8))).T.reshape(-1).astype(np.float64)
CODE_VALUE, SCALE_VALUE = values_of_codes(), 2.0 ** (np.arange(256) - 127.0)
def decode(q):
    return (CODE_VALUE[q[0]].reshape(16, 8, -1, 4) * SCALE_VALUE[q[1]][:, None, :, None] + 0.0).reshape(128, -1).astype(np.float32)
def f(rng, *shape):
    return mx_ref.flush((rng.standard_normal(shape, dtype=np.float32) * np.exp2(rng.integers(-2, 3, shape[:-1] + (1,)))).astype(BF))
def wide(rng, *shape, cols=0):
    v = rng.standard_normal(shape, dtype=np.float32) * np.exp2(rng.integers(-12, 13, shape)).astype(np.float32)
    if cols: v *= np.repeat(np.exp2(rng.integers(-cols, cols + 1, shape[:-2] + (1, shape[-1] // 4))) * (rng.random(shape[:-2] + (1, shape[-1] // 4)) > 0.0625), 4, axis=-1).astype(np.float32)
    return mx_ref.flush(v.astype(BF))
C, B, R = 320, 96, 3
def order(p):
    return np.argsort(-(p[::16] + np.float32(0.0)), axis=1, kind="stable")
def big(v):
    v = v.astype(np.float32)
    v[np.abs(v) < np.float32(2.0 ** -16)] = 0
    return v.astype(BF)
def numbers_of(rng):
    return {"x": big(f(rng, N, 128, 16 * C)), "u": np.array(f(rng, N, 128, 512)), "v": np.array(f(rng, N, 128, 512))}
def weights(rng, kept=[]):
    w = np.array(f(rng, N, 128, 2048)).reshape(N, 8, 16, 4, 8, 16, 4)
    for i in kept:
        w[:, :, i] = 0
        w[:, :, :, :, :, i] = 0
        for g in range(8):
            for k in range(4): w[:, g, i, k, g, i, k] = 32
    c, p = packed(w.reshape(N, 128, 2048), rng)
    return {"wc": c, "ws": p}
def paths(rng):
    a = np.zeros((N, 8, C), int)
    for r in range(N):
        for g in range(8):
            a[r, g, ::2] = rng.permutation(C // 2) * 2 + 1
            a[r, g, 1::2] = rng.permutation(C // 2) * 2
    return [a, rng.integers(0, B, (N, 8, C)), rng.integers(0, 4, (N, 8, C)), rng.integers(0, 4, (N, 8, C))]
def stored(p):
    return {k: np.stack([gtable(e[r]) for r in range(N)]) for k, e in zip(("la", "lb", "da", "db"), p)}
def plant(rng, p, z):
    x = np.zeros((N, 8, 16, 4, C, 4), np.float32)
    at = np.zeros((N, 8, C), int)
    for r in range(N):
        for g in range(8):
            a = p[0][r, g]
            at[r, g, a] = p[2][r, g]
            x[r, g][:, :, a] = z[r, g][:, None]
            x[r, g][:, :, :B][:, np.arange(4)[:, None] != at[r, g, :B]] = 0
    for r in range(N): p[3][r] = (np.take_along_axis(at[r - 1], p[1][r], axis=1) + rng.integers(1, 4, (8, C))) % 4
    return x.reshape(N, 128, 16 * C).astype(BF)
def signs(rng):
    return np.stack([rng.permutation(8) % 2 * 2.0 - 1.0 for r in range(N)])
def setup_inputs(rng):
    return {**numbers_of(rng), **weights(rng), **stored(paths(rng))}
def setup_inputs_ties(rng):
    d = numbers_of(rng)
    e = rng.permutation(N)
    x = d["x"].reshape(N, 8, 16, 4, C, 4)
    for r in range(N):
        k = np.zeros((4, C), int) if r == e[0] else rng.integers(0, 3, (4, C))
        a = x[r][:, :8, 0, :3].copy()
        a[:, :, 2] = 0
        x[r][:, :8] = a[:, :, k]
    x[e[1]] = 0
    u = d["u"].reshape(N, 8, 16, 8, 16, 4)
    k = u.copy()
    u[:, :, :, :, :2] = 0
    for g in range(8): u[:, g, :8, g, :2] = k[:, g, :8, g, :2]
    return {"x": x.reshape(N, 128, 16 * C), "u": u.reshape(N, 128, 512), "v": d["v"], **weights(rng, range(8)), **stored(paths(rng))}
def setup_inputs_near(rng):
    d = numbers_of(rng)
    p = paths(rng)
    z = np.zeros((N, 8, 16, C, 4), np.float32)
    u = d["u"].reshape(N, 128, 128, 4)
    u[:, :, ::16] = 0
    u[:, :, 1::16] = 0
    o, c = rng.permutation(N) % 4, signs(rng)
    upper = np.arange(C) // (C // 2)
    for r in range(N):
        i = (np.arange(C) + rng.integers(0, C, (8, 1))) % C
        if o[r] == 3: i = i % (C // 2) * 2 + upper
        s = (i + 1) // 2
        size = 1.0 if o[r] < 2 else 2.0 ** -4
        m = ((s[:, :, None] >> np.arange(8)) & 1) * np.exp2(np.arange(8) - 22.0) * size
        if o[r] < 2:
            z[r, :, 0, :, 0] = 2 * c[r][:, None]
            for g in rng.permutation(8)[:4]: z[r, g, 0, rng.integers(C), 0] *= np.float32(2.0 ** 29)
        if o[r] == 3: z[r, :, 0, :, 0] = (8 + upper) * 2.0 ** -29
        z[r, :, 1, :, 0] = rng.integers(-1, 2, (8, C)) * (2.0 if o[r] < 2 else 2.0 ** -26)
        z[r, :, 8] = m[:, :, :4]
        z[r, :, 9] = m[:, :, 4:]
        z[r, :, 10:] = rng.integers(4, 8, (8, 6, C, 4)) * 2.0 ** -19 * size
        k = 1.0 if o[r] == 0 else 2.0 ** -30
        for h in range(0, 128, 16):
            u[r, h, h, 0] = k
            u[r, h + 8:h + 10, h] = k
            u[r, h + 1, h + 1, 0] = k
    x = plant(rng, p, z)
    return {"x": x, "u": u.reshape(N, 128, 512), "v": d["v"], **weights(rng, range(16)), **stored(p)}
def setup_inputs_lags(rng):
    d = numbers_of(rng)
    p = paths(rng)
    p[2] = rng.integers(1, 3, (N, 8, C))
    x = d["x"].astype(np.float32).reshape(N, 8, 16, 4, C, 4)
    u = d["u"].reshape(N, 128, 128, 4)
    u[:, :, 1::16] = 0
    kind = rng.permutation(8)
    ends = [(3, 3), (0, 0), (9, 9), (9, 9), (9, 0), (9, 3), (3, 9), (9, 9)]
    for g in range(8):
        k = kind[g]
        x[:, g, 0, :, :, 0] = rng.integers(4, 8, (N, 4, C)) * 0.25 * [1, -1, 1, -1, 1, -1, 1, 0][k]
        u[:, 16 * g, 16 * g + 1, 0] = 1
        for i in range(2):
            if ends[k][i] < 9: p[2][:, g, i::2] = ends[k][i]
        if k == 2: p[0][:, g] = np.arange(C) ^ 1
        if k == 3: p[0][:, g] = (np.arange(C) + 1) % C
        if k == 4: p[1][:, g], p[3][:, g] = rng.integers(B), 0
        if k == 5: p[3][:, g] = 3
    return {"x": x.reshape(N, 128, 16 * C).astype(BF), "u": u.reshape(N, 128, 512), "v": d["v"], **weights(rng, [0]), **stored(p)}
def setup_inputs_huge(rng):
    d = numbers_of(rng)
    p = paths(rng)
    c = np.stack([rng.permutation(C) % 2 * 2.0 - 1.0 for r in range(N)])
    c[rng.permutation(N) < N // 2] = -1
    z = 2.0 ** 30 * (0.8 + 0.2 * rng.random((N, 8, 16, C, 4))) * c[:, None, None, :, None]
    x = plant(rng, p, z.astype(np.float32))
    u = d["u"].reshape(N, 128, 8, 16, 4)
    a = 2.0 ** 30 * (1 - 0.1 * rng.random((N, 128, 8, 2, 4))) * np.stack([signs(rng), signs(rng)], axis=2)[:, None, :, :, None]
    u[:, :, :, :2] = a.astype(np.float32).astype(BF)
    return {"x": x, "u": u.reshape(N, 128, 512), "v": d["v"], **weights(rng, range(16)), **stored(p)}
def setup_inputs_spread(rng):
    d = setup_inputs(rng)
    d["x"] = big(wide(rng, N, 128, 16 * C, cols=6))
    return d
def check_inputs(d):
    b = []
    for k in ("x", "u", "v"):
        a = np.abs(d[k].astype(np.float32))
        if not (np.isfinite(a).all() and ((a == 0) | (a >= 2.0 ** -30) & (a <= 2.0 ** 30)).all()): b.append("a value of " + k)
    none, least, most = [emit(mx_ref.quantize(np.full((128, 16), k, np.float32).astype(BF)))[1][0, 0] for k in (0.0, 2.0 ** -30, 2.0 ** 30)]
    for r in range(N):
        if ((d["wc"][r] == 0x7F) | (d["wc"][r] == 0xFF)).any(): b.append("wc: a code that is no number")
        s = mx_ref.live(d["ws"][r])
        if ((s != none) & ((s < least) | (s > most))).any(): b.append("ws: a scale out of range")
        a = gentries(d["la"][r])
        if (np.sort(a, axis=1) != np.arange(C)).any(): b.append("la: no permutation")
        if ((a + np.arange(C)) % 2 != 1).any(): b.append("la: a number of the same parity")
        for k, n in (("lb", B), ("da", 4), ("db", 4)):
            if ((d[k][r] < 0) | (d[k][r] >= n)).any(): b.append(k + " out of range")
    return b
def reference(x, u, v, wc, ws, la, lb, da, db):
    qu = [mx_ref.quantize(u[r]) for r in range(N)]
    lay = [pk(wc[r], ws[r]) for r in range(N)]
    ring = [x[r] for r in range(N)]
    came = decode(join(*[mx_ref.quantize(np.ascontiguousarray(x[r].reshape(128, 4, C, 4)[:, :, :B]).reshape(128, -1)) for r in range(N)])).astype(BF)
    edge = [cut(came, (r - 1) % N, 16 * B) for r in range(N)]
    lag = np.zeros((N, 8, C), np.int64)
    last = [None] * N
    for t in range(R):
        sent = []
        for r in range(N):
            a = gentries(la[r])
            delay = gentries(da[r]) + lag[r] - np.take_along_axis(lag[r], a, axis=1)
            own = gcols(ring[r], C * delay + a)
            far = gcols(edge[r], B * gentries(db[r]) + gentries(lb[r]))
            q = mx_ref.quantize(((own.astype(np.float32) + far.astype(np.float32)) * np.float32(0.5)).astype(BF))
            s = mx_ref.matmul(qu[r], q)
            h = tile([mx_ref.matmul(pick(lay[r], np.arange(128 * b, 128 * b + 128)), q) * np.float32(0.03125) for b in range(4)])
            last[r] = h
            ring[r] = np.concatenate([h, ring[r][:, :12 * C]], axis=1)
            sent.append(mx_ref.quantize(gcols(h, order(s)[:, :B])))
            step = ((s[1::16] > 0).astype(np.int64) - (s[1::16] < 0)) * (np.arange(C) % 2 == t % 2)
            one = delay + step
            two = np.take_along_axis(delay, np.argsort(a, axis=1), axis=1) - step
            lag[r] += np.where((one >= 0) & (one <= 3) & (two >= 0) & (two <= 3), step, 0)
        if t < R - 1:
            came = decode(join(*sent)).astype(BF)
            edge = [np.concatenate([cut(came, (r - 1) % N, 4 * B), edge[r][:, :12 * B]], axis=1) for r in range(N)]
    y, ol = np.zeros((N, 128, C), np.float32), np.zeros((N, 8, C), np.float32)
    oc, osc = np.zeros((N, 128, 4 * C), np.uint8), np.zeros((N, 16, C), np.uint8)
    for r in range(N):
        q = mx_ref.quantize(last[r])
        y[r] = mx_ref.matmul(mx_ref.quantize(v[r]), q)
        ol[r] = lag[r]
        oc[r], osc[r] = emit(q)
    return {"y": y, "ol": ol, "oc": oc, "osc": osc}

@@ -1,0 +1,525 @@
+from concourse.mybir import dt, AluOpType, ActivationFunctionType
+
+C, B, R = 320, 96, 3
+LV = 4 * C
+HC = C // 2
+BIG = 1.0e29
+SP = (19, 18, 17, 16, 15)
+F8 = "float8_e4m3fn_x4"
+TILES = [(0, 320, (0, 19, 18, 17)), (1280, 256, (16, 15, 14, 13)), (2304, 192, (12, 11, 10, 9)),
+         (3072, 128, (8, 7, 6, 5)), (3584, 128, (4, 3, 2, 1))]
+WIDTHS = {
+    "bfloat16": dict(ring=6 * LV, xb=16 * B, bord=24 * B, ownh=LV, z=LV, hl=LV, gt=512, ub=512, vb=512, eb=520, ob=512,
+                     ct=4096, sgn2=20 * C, m16=16, d128=128, c16=128, tab=16, m01=C, keep=C, msg=C, dbb=C, mpp=C, spp=C,
+                     seg=C, sgn=C, ml=C, sl=C),
+    F8: dict(qx=4 * B, lq=6 * B, qz=C, qh=C, qg=256, qu=128, qup=256, qv=128, qw=512, qe=640, qc=1024),
+    "uint8": dict(sx=4 * B, ls=6 * B, sz=C, sh=C, sg=256, su=128, sup=256, sv=128, sw=512, se=640, sc=1024),
+    "float32": dict(rs=20, pf=8, r16=16, i4=C, k16=20, r4=B, tabl=50, mbig=C, kk=C, m4=B, keep4=B, base=20, lf=80, a44=40,
+                    dl=60, ds=20, ph=40, cb=C, mc=C, oc4=C, pa=80, pb=40, pc=80, sm=20, hlo=40, hla=40, mp=C, oh=C,
+                    t1=20, rp=20, m2=C, o2=C, rk=20, ee=C, me=B, oe=B, n1=20, n2=20, e0=20, w0=60, lm=20, l3=60,
+                    lb3=3 * C, f1=HC, f2=HC, ysb=C),
+    "int32": dict(pi=1, pw=8, poi=16, li=80),
+    "uint16": dict(qo=20, po=16, au=20, d5=20, oo=80, fo=20, pu=80, ru=20, go=24, l3u=60),
+}
+SCRATCH = {k: ("sbuf", [128, n], d) for d, v in WIDTHS.items() for k, n in v.items()}
+SCRATCH["ps"] = ("psum", [128, 4096], "float32")
+SEMAPHORES = ["cv", "cs", "cp", "cg", "dxa", "dxb", "dli", "dxr", "du", "dw", "dv", "dout",
+              "arr0", "arr1", "arr2", "arr3", "snt"]
+COUNTER = {"v": "cv", "s": "cs", "p": "cp", "g": "cg"}
+
+
+def schedule(ops, queues, T):
+    hist, known, seq, group = {}, {}, {}, {}
+    for n, o in enumerate(ops):
+        deps = set(o["after"])
+        for acc, wr in [(a, False) for a in o["r"]] + [(a, True) for a in o["w"]]:
+            name, cols = acc
+            for m, c2, w2 in hist.get(name, []):
+                if m == n or not (cols & c2):
+                    continue
+                other = ops[m]["q"] != o["q"]
+                if name == "ps" and not other and o["q"] == "p":
+                    continue
+                if wr or w2 or (name == "ps" and other):
+                    deps.add(m)
+            hist.setdefault(name, []).append((n, cols, wr))
+        kn = known.setdefault(o["q"], {})
+        need = {}
+        for m in deps:
+            d = ops[m]
+            key = d["sem"] or d["q"]
+            lvl = 1 if d["sem"] else d["seq"]
+            if kn.get(key, 0) < lvl and need.get(key, (0, 0))[0] < lvl:
+                need[key] = (lvl, m)
+        waits = []
+        for key, (lvl, m) in sorted(need.items(), key=lambda kv: -kv[1][1]):
+            if kn.get(key, 0) >= lvl:
+                continue
+            waits.append(m)
+            ops[m]["inc"] = True
+            for mm in (group[key] if ops[m]["sem"] else [m]):
+                for k2, l2 in ops[mm]["clock"].items():
+                    kn[k2] = max(kn.get(k2, 0), l2)
+            kn[key] = lvl
+        o["waits"] = waits
+        o["clock"] = dict(kn)
+        if o["sem"]:
+            group.setdefault(o["sem"], []).append(n)
+        else:
+            seq[o["q"]] = seq.get(o["q"], 0) + 1
+            o["seq"] = seq[o["q"]]
+    count = {}
+    for o in ops:
+        if not o["sem"] and o["inc"]:
+            count[o["q"]] = count.get(o["q"], 0) + 1
+            o["count"] = count[o["q"]]
+    for o in ops:
+        if o["fn"] is None:
+            continue
+        q = queues[o["q"]]
+        for m in o["waits"]:
+            d = ops[m]
+            if d["sem"]:
+                q.wait_ge(T.sem[d["sem"]], sum(ops[k]["n"] for k in group[d["sem"]]))
+            else:
+                q.wait_ge(T.sem[COUNTER[d["q"]]], d["count"])
+        ins = o["fn"]()
+        if o["sem"] and o["dma"]:
+            ins.then_inc(T.sem[o["sem"]], 16)
+        elif o["inc"] and not o["sem"]:
+            ins.then_inc(T.sem[COUNTER[o["q"]]], 1)
+    return {k: sum(ops[m]["n"] for m in v) for k, v in group.items()}
+
+
+def rank_program(g, core, T, topo):
+    rank = T.rank_of(core)
+    if rank is None:
+        return
+    A, AF = AluOpType, ActivationFunctionType
+    nxt = T.cores[(rank + 1) % len(T.cores)]
+    prv = T.cores[(rank - 1) % len(T.cores)]
+    rid, pid, _se = topo.addr(nxt)
+    out_mask = topo.mask(core, nxt)
+    n_out = len(topo.engines(core, nxt))
+    n_in = len(topo.engines(prv, core))
+    V, S, P, Y = g.vector, g.scalar, g.tensor, g.sync
+    queues = {"v": V, "s": S, "p": P, "y": Y, "g": g}
+    ops = []
+
+    def a(name, lo=0, hi=None, step=1):
+        if hi is None:
+            hi = SCRATCH[name][1][1]
+        if name == "ps":
+            cols = set(range(lo // 512, (hi - 1) // 512 + 1))
+        else:
+            cols = set(range(lo, hi, step))
+        view = T[name][:, lo:hi] if step == 1 else T[name][:, lo:hi:step]
+        return (view, [(name, cols)])
+
+    def ind(win, off):
+        return (win[0].indirect(off[0]), win[1] + off[1])
+
+    def bank(b, lo=0, hi=C, step=1):
+        return a("ps", 512 * b + lo, 512 * b + hi, step)
+
+    def add(q, fn, r=(), w=(), sem=None, n=16, dma=True, after=()):
+        rr, ww = [], []
+        for x in r:
+            if isinstance(x, tuple):
+                rr += x[1]
+        for x in w:
+            ww += x[1]
+        ops.append({"q": q, "fn": fn, "r": rr, "w": ww, "sem": sem, "n": n, "dma": dma, "after": list(after), "inc": False})
+        return len(ops) - 1
+
+    def val(x):
+        return x[0] if isinstance(x, tuple) else x
+
+    def tt(o, x, y, op):
+        return add("v", lambda: V.tensor_tensor(o[0], x[0], y[0], op), [x, y], [o])
+
+    def ts(o, x, s1, op0, s2=None, op1=None):
+        if op1 is None:
+            return add("v", lambda: V.tensor_scalar(o[0], x[0], val(s1), None, op0), [x, s1], [o])
+        return add("v", lambda: V.tensor_scalar(o[0], x[0], val(s1), val(s2), op0, op1), [x, s1, s2], [o])
+
+    def cp(o, x):
+        return add("v", lambda: V.tensor_copy(o[0], x[0]), [x], [o])
+
+    def scatter(win, off, x):
+        return add("v", lambda: V.tensor_copy(win[0].indirect(off[0]), x[0]), [x, off], [win])
+
+    def ms(o, c):
+        return add("v", lambda: V.memset(o[0], c), [], [o])
+
+    def scan(o, d0, d1, init, op0, op1):
+        return add("v", lambda: V.tensor_tensor_scan(o[0], d0[0], d1[0], init, op0, op1), [d0, d1], [o])
+
+    def quant(q, s, lo, hi, x):
+        qq, ss = a(q, lo, hi), a(s, lo, hi)
+        return add("v", lambda: V.quantize_mx(qq[0], ss[0], x[0]), [x], [qq, ss])
+
+    def act(o, x, f, bias=None, scale=None, acc=None):
+        kw = {}
+        if bias is not None:
+            kw["bias"] = val(bias)
+        if scale is not None:
+            kw["scale"] = val(scale)
+        if acc is not None:
+            kw["accum_out"] = acc[0]
+        return add("s", lambda: S.activation(o[0], x[0], f, **kw), [x, bias, scale], [o] + ([acc] if acc else []))
+
+    def mm(b, lq, ls, at, rq, rs, lo, hi, start=True, stop=True):
+        o, v = bank(b, 0, hi - lo), [a(lq, at, at + 128), a(ls, at, at + 128), a(rq, lo, hi), a(rs, lo, hi)]
+        return add("p", lambda: P.matmul_mx(o[0], v[0][0], v[1][0], v[2][0], v[3][0], start, stop), v, [o])
+
+    def iota(o, pat, base=0, cm=0, small=True):
+        if small:
+            return add("g", lambda: g.iota(o[0], pat, base, cm, allow_small_or_imprecise_dtypes=True), [], [o])
+        return add("g", lambda: g.iota(o[0], pat, base, cm), [], [o])
+
+    def load(q, sem, o, src, after=(), codes=False):
+        dst = o[0].bitcast(dt.uint8) if codes else o[0]
+        return add(q, lambda: queues[q].dma_start(dst, src), [], [o], sem=sem, after=after)
+
+    def store(q, dst, view, x):
+        return add(q, lambda: queues[q].dma_start(dst, view), [x], [], sem="dout")
+
+    def send(sem, name, x, lo, hi):
+        if name == "lq":
+            dst, src = T.lq[:, lo:hi].bitcast(dt.uint8), x[0].bitcast(dt.uint8)
+        else:
+            dst, src = T.ls[:, lo:hi], x[0]
+        add("g", lambda: g.remote_dma(dst, src, T.sem[sem], T.sem.snt, pid, rid, out_mask), [x], [], sem="snt",
+            n=n_out, dma=False)
+        add("x", None, [], [a(name, lo, hi)], sem=sem, n=n_in)
+
+    def scaled(q, dst, src, c):
+        if q == "v":
+            ts(dst, src, c, A.mult)
+        else:
+            act(dst, src, AF.Identity, scale=c)
+
+    col = lambda name, j: a(name, j, j + 1)
+    ends = lambda name: a(name, 15, C, 16)
+    Q16, GRP, ODD, T4, Q4, EVEN, SIG = [col("pf", j) for j in range(7)]
+    X0 = 2 * LV
+
+    for k in range(4):
+        load("ys"[k % 2], "dxa" if k < 2 else "dxb", a("xb", 4 * B * k, 4 * B * (k + 1)), T.x[:, LV * k:LV * k + 4 * B])
+    for j, t in enumerate((T.la, T.lb, T.da, T.db)):
+        load("ys"[j % 2], "dli", a("li", 20 * j, 20 * j + 20), t[:])
+    load("s", "du", a("ub"), T.u[:])
+    xr = [load("y", "dxr", a("ring", X0 + LV * k + 4 * B, X0 + LV * (k + 1)), T.x[:, LV * k + 4 * B:LV * (k + 1)])
+          for k in range(4)]
+    load("y", "dw", a("qw"), T.wc[:], after=xr, codes=True)
+    load("y", "dw", a("sw"), T.ws[:])
+    load("y", "dv", a("vb"), T.v[:])
+
+    iota(a("pi"), [[0, 1]], 0, 1, small=False)
+    iota(a("d128"), [[1, 128]], 0, -1)
+    iota(a("r16"), [[1, 16]])
+    iota(a("k16"), [[16, 20]])
+    iota(a("poi"), [[1, 2], [16, 8]], small=False)
+    iota(a("tab"), [[256, 16]])
+    iota(a("i4"), [[4, C]])
+    ms(a("eb"), 0.0)
+    ts(col("pw", 0), a("pi"), 15, A.bitwise_and)
+    ts(col("pw", 1), a("pi"), 4, A.logical_shift_right)
+    ts(col("pw", 2), a("pi"), 1, A.bitwise_and)
+    ts(col("pw", 3), a("pi"), 3, A.bitwise_and)
+    ts(col("pw", 4), a("pi"), 2, A.logical_shift_right, 3, A.bitwise_and)
+    ts(a("eb", 3, 515, 4), a("d128"), 0.0, A.is_equal)
+    cp(a("pf", 0, 5), a("pw", 0, 5))
+    ms(a("keep"), 1.0)
+    ts(a("m16"), a("r16"), Q16, A.is_equal)
+    ts(a("qo"), a("k16"), 0.0, A.mult, Q16, A.add)
+    ts(EVEN, ODD, -1.0, A.mult, 1.0, A.add)
+    ts(SIG, ODD, -2.0 * LV, A.mult, float(LV), A.add)
+    ms(a("keep", 0, C, 16), 0.0)
+    for b in range(4):
+        quant("qe", "se", 128 * b, 128 * b + 128, a("eb", 3 - b, 515 - b))
+    for lo, n, planes in TILES:
+        ms(a("ct", lo + 4 * 16 * planes[3], lo + 4 * n), 0.0)
+    act(a("m01"), ind(a("m16"), a("qo")), AF.Copy)
+    act(a("mbig"), a("m01"), AF.Identity, bias=-BIG, scale=2 * BIG)
+    act(a("kk"), a("m01"), AF.Identity, bias=BIG, scale=-2 * BIG)
+    act(a("msg"), a("m01"), AF.Identity, scale=SIG)
+
+    quant("qx", "sx", 0, 2 * B, a("xb", 0, 8 * B))
+    send("arr0", "lq", a("qx", 0, 2 * B), 0, 2 * B)
+    ms(a("gt", 4 * B, 512), 0.0)
+    ms(col("rs", 0), 0.0)
+    cp(a("po"), a("poi"))
+    ts(a("pa", 40, 60), a("k16"), Q16, A.add, EVEN, A.mult)
+    ts(a("pa", 60, 80), a("k16"), Q16, A.add, ODD, A.mult)
+    ts(a("base"), a("k16"), Q16, A.subtract, 15.0, A.add)
+    ms(a("kk", 0, C, 16), -BIG)
+    quant("qx", "sx", 2 * B, 4 * B, a("xb", 8 * B, 16 * B))
+    send("arr0", "ls", a("sx"), 0, 4 * B)
+    send("arr3", "lq", a("qx", 2 * B, 4 * B), 2 * B, 4 * B)
+    iota(a("c16"), [[1, 8], [0, 16]])
+    iota(a("r4"), [[0, 24], [1, 4]])
+    iota(a("tabl"), [[1, 10], [0, 5]], -4)
+    for k in range(4):
+        act(a("ring", X0 + LV * k, X0 + LV * k + 4 * B), a("xb", 4 * B * k, 4 * B * (k + 1)), AF.Copy)
+
+    cp(a("au"), a("li", 0, 20))
+    cp(a("lf"), a("li"))
+    scatter(a("cb"), a("au"), a("i4"))
+    ts(a("ds"), a("lf", 40, 60), float(LV), A.mult)
+    ts(a("a44", 0, 20), a("lf", 0, 20), 4.0, A.mult)
+    ts(a("d5"), a("ds"), 1.0 / 256, A.mult)
+    tt(a("dl", 0, 20), a("ds"), a("a44", 0, 20), A.add)
+    tt(a("mc"), a("cb"), a("m01"), A.mult)
+    for t in range(4):
+        ts(a("oo", 20 * t, 20 * t + 20), a("dl", 0, 20), float(t), A.add)
+    scan(a("oc4"), a("keep"), a("mc"), 0.0, A.mult, A.add)
+    ts(a("pb", 0, 20), a("lf", 0, 20), ODD, A.mult)
+    ts(a("pb", 20, 40), a("lf", 0, 20), EVEN, A.mult)
+    ts(a("pa", 0, 20), ends("oc4"), 0.25, A.mult, EVEN, A.mult)
+    ts(a("pa", 20, 40), ends("oc4"), 0.25, A.mult, ODD, A.mult)
+    tt(a("pc", 40, 80), a("pa", 40, 80), a("pb"), A.add)
+    ts(a("ph", 0, 20), a("lf", 60, 80), float(B), A.mult)
+    tt(a("pc", 0, 40), a("pa", 0, 40), a("pb"), A.add)
+    tt(a("ph", 20, 40), a("ph", 0, 20), a("lf", 20, 40), A.add)
+    ts(a("a44", 20, 40), a("lf", 0, 20), 4.0, A.mult)
+    cp(a("pu"), a("pc"))
+    cp(a("fo"), a("ph", 20, 40))
+    quant("qu", "su", 0, 128, a("ub"))
+
+    def delays_out():
+        act(a("dbb"), ind(a("tab"), a("d5")), AF.Copy)
+
+    def own(r, t, q):
+        src = ind(a("ring", (2 - r) * LV, (6 - r) * LV), a("oo", 20 * t, 20 * t + 20))
+        scaled(q, a("ownh", C * t, C * t + C), src, 0.5)
+
+    def partner_pick(r):
+        tt(a("mpp"), ind(a("dbb"), a("pu", 20 * (r % 2), 20 * (r % 2) + 20)), a("m01"), A.mult)
+
+    def partner_scan():
+        scan(a("spp"), a("keep"), a("mpp"), 0.0, A.mult, A.add)
+
+    def bounds_sum():
+        tt(a("sm"), ends("spp"), a("ds"), A.add)
+
+    def bounds():
+        ts(a("hlo", 0, 20), a("sm"), 3.0 * LV, A.min)
+        ts(a("hlo", 20, 40), a("sm"), 3.0 * LV, A.subtract, 0.0, A.max)
+
+    def bounds_shift():
+        tt(a("hla"), a("hlo"), a("a44"), A.add)
+
+    def unpack(lo, n, at, first, who, order):
+        w = max(n, 128)
+        for b in order:
+            mm(first + b, "qe", "se", 128 * b, "lq", "ls", lo + n - w, lo + n)
+        for b in order:
+            scaled(who[b], a("bord", 6 * B * b + at, 6 * B * b + at + n), bank(first + b, w - n, w), 0.5)
+
+    def reading(r, order, lo=0, hi=C):
+        for t in order:
+            win = a("bord", 6 * B * t + (2 - r) * B, 6 * B * t + (6 - r) * B)
+            tt(a("z", 4 * lo + t, 4 * hi, 4), ind(win, a("fo", lo // 16, hi // 16)), a("ownh", C * t + lo, C * t + hi), A.add)
+        quant("qz", "sz", lo, hi, a("z", 4 * lo, 4 * hi))
+
+    place = {}
+    for lo, n, planes in TILES:
+        for t, k in enumerate(planes):
+            place[k] = lo + t
+
+    def plane(k):
+        return a("ct", place[k], place[k] + 4 * (16 * k if k else C) - 3, 4)
+
+    def score(k):
+        return col("oh", 16 * k + 15)
+
+    def compare(ks):
+        for k in ks:
+            if k not in SP:
+                ts(plane(k), bank(0, 0, 16 * k), score(k), A.is_lt)
+
+    def pack(m):
+        lo, n, _p = TILES[m]
+        quant("qc", "sc", lo // 4, lo // 4 + n, a("ct", lo, lo + 4 * n))
+
+    def count(m, start, stop):
+        lo, n, _p = TILES[m]
+        mm(3, "qe", "se", 512, "qc", "sc", lo // 4, lo // 4 + n, start, stop)
+
+    delays_out()
+    add("s", lambda: S.activation(T.sup[:, 0:256], T.su[:, 0:128].indirect(T.po[:, 0:16]), AF.Copy),
+        [a("su"), a("po")], [a("sup")])
+    partner_pick(0)
+    add("v", lambda: V.tensor_copy(T.qup[:, 0:256].bitcast(dt.uint32),
+                                   T.qu[:, 0:128].bitcast(dt.uint32).indirect(T.po[:, 0:16])),
+        [a("qu"), a("po")], [a("qup")])
+    partner_scan()
+    for t in range(4):
+        ts(a("ob", t, 512, 4), a("c16"), GRP, A.is_equal)
+    bounds_sum()
+    ts(a("m4"), a("r4"), Q4, A.is_equal)
+    bounds()
+    quant("qe", "se", 512, 640, a("ob"))
+    bounds_shift()
+    act(a("keep4"), a("r4"), AF.Sign)
+    order = (0, 1, 2, 3)
+    for t in order:
+        own(0, t, "s")
+    unpack(0, 2 * B, 2 * B, 4, "vvvv", order)
+    unpack(2 * B, 2 * B, 4 * B, 0, "vsss", order)
+    CUT = 16 * min(SP[:4])
+
+    for r in range(R - 1):
+        at = (1 - r) * LV
+        reading(r, order)
+        mm(0, "qup", "sup", 0, "qz", "sz", 0, C)
+        mm(1, "qup", "sup", 0, "qz", "sz", 0, C)
+        for b in range(4):
+            mm(4 + b, "qw", "sw", 128 * b, "qz", "sz", 0, C)
+        mm(2, "qup", "sup", 128, "qz", "sz", 0, C)
+        if r == 1:
+            tt(a("e0"), a("dl", 20, 40), a("dl", 0, 20), A.subtract)
+            ts(a("w0", 20, 40), a("dl", 20, 40), ODD, A.mult)
+            ts(a("w0", 0, 20), a("e0"), EVEN, A.mult)
+        tt(a("mp", CUT, C), bank(0, CUT, C), a("mbig", CUT, C), A.min)
+        scan(a("oh", CUT, C), a("kk", CUT, C), a("mp", CUT, C), -BIG, A.min, A.max)
+        tt(a("mp", 0, CUT), bank(0, 0, CUT), a("mbig", 0, CUT), A.min)
+        if r == 1:
+            tt(a("w0", 40, 60), a("w0", 0, 20), a("w0", 20, 40), A.subtract)
+        scan(a("oh", 0, CUT), a("kk", 0, CUT), a("mp", 0, CUT), -BIG, A.min, A.max)
+        for j in range(len(SP) + 1):
+            if j < len(SP):
+                k = SP[j]
+                act(a("sgn2", C * k, C * k + 16 * k), bank(1, 0, 16 * k), AF.Sign, bias=score(k), scale=-1.0)
+            if j > 0:
+                k = SP[j - 1]
+                act(plane(k), a("sgn2", C * k, C * k + 16 * k), AF.Relu, acc=col("rs", k))
+        compare((19, 18, 17, 16, 15, 14, 13))
+        tt(plane(0), a("oh"), bank(0), A.is_ge)
+        compare((12, 11, 10, 9))
+        scan(a("seg"), a("keep"), plane(0), 0.0, A.mult, A.add)
+        pack(0)
+        compare((8, 7, 6, 5))
+        pack(2)
+        tt(a("t1"), a("base"), ends("seg"), A.subtract)
+        compare((4, 3, 2, 1))
+        pack(1)
+        pack(3)
+        pack(4)
+        for j, m in enumerate((0, 2, 1, 3, 4)):
+            count(m, j == 0, j == 4)
+        for k in range(19, 0, -1):
+            if k not in SP:
+                act(a("sgn2", C * k, C * k + 16 * k), plane(k), AF.Copy, acc=col("rs", k))
+        for b in range(4):
+            scaled("s", a("ring", at + b, at + LV, 4), bank(4 + b), 0.03125)
+        act(a("sgn"), bank(2), AF.Sign)
+        tt(a("m2"), bank(3), a("mbig"), A.min)
+        scan(a("o2"), a("kk"), a("m2"), -BIG, A.min, A.max)
+        tt(a("rp"), a("t1"), a("rs"), A.subtract)
+        tt(a("rk"), ends("o2"), a("rp"), A.add)
+        cp(a("ru"), a("rk"))
+        scatter(a("ee"), a("ru"), a("i4"))
+        tt(a("me"), a("ee", 0, B), a("m4"), A.mult)
+        scan(a("oe"), a("keep4"), a("me"), 0.0, A.mult, A.add)
+        ts(a("go"), a("oe", 3, B, 4), T4, A.add)
+        h = a("ring", at, at + LV)
+        act(a("gt", 2 * B, 4 * B), ind(h, a("go", 12, 24)), AF.Copy)
+        cp(a("gt", 0, 2 * B), ind(h, a("go", 0, 12)))
+        quant("qg", "sg", 128 * r, 128 * r + 128, a("gt"))
+        send("arr%d" % (r + 1), "lq", a("qg", 128 * r, 128 * r + B), (4 + r) * B, (5 + r) * B)
+        send("arr%d" % (r + 1), "ls", a("sg", 128 * r, 128 * r + B), (4 + r) * B, (5 + r) * B)
+        tt(a("ml"), ind(a("sgn"), a("pu", 40 + 20 * r, 60 + 20 * r)), a("msg"), A.mult)
+        scan(a("sl"), a("keep"), a("ml"), 0.0, A.mult, A.add)
+        old, new = a("dl", 20 * r, 20 * r + 20), a("dl", 20 * r + 20, 20 * r + 40)
+        tt(a("n1"), old, ends("sl"), A.add if r == 0 else A.subtract)
+        tt(a("n2"), a("n1"), a("hla", 0, 20), A.min)
+        tt(new, a("n2"), a("hla", 20, 40), A.max)
+        tt(a("ds"), new, a("a44", 0, 20), A.subtract)
+        ts(a("oo", 40, 60), new, 2.0, A.add)
+        ts(a("d5"), a("ds"), 1.0 / 256, A.mult)
+        ts(a("oo", 0, 20), new, 0.0, A.add)
+        ts(a("oo", 60, 80), new, 3.0, A.add)
+        ts(a("oo", 20, 40), new, 1.0, A.add)
+        delays_out()
+        own(r + 1, 2, "s")
+        own(r + 1, 3, "s")
+        own(r + 1, 1, "s")
+        own(r + 1, 0, "v")
+        order = (0, 2, 3, 1)
+        partner_pick(r + 1)
+        if r == 0:
+            quant("qv", "sv", 0, 128, a("vb"))
+            partner_scan()
+            bounds_sum()
+            bounds()
+            bounds_shift()
+        else:
+            ts(a("e0"), new, ODD, A.mult)
+            partner_scan()
+            tt(a("lm"), a("w0", 0, 20), a("ds"), A.subtract)
+            bounds_sum()
+            tt(a("l3", 0, 20), a("e0"), a("w0", 40, 60), A.add)
+            bounds()
+            tt(a("l3", 20, 40), a("hlo", 0, 20), a("lm"), A.add)
+            tt(a("l3", 40, 60), a("hlo", 20, 40), a("lm"), A.add)
+            ts(a("l3u"), a("l3"), 1.0 / 256, A.mult, 20.0, A.add)
+        unpack((4 + r) * B, B, (1 - r) * B, 4, "vsss", order)
+
+    act(a("lb3"), ind(a("tabl"), a("l3u")), AF.Copy)
+    banks = ((4, 5, 6, 7, 2, 4), (0, 1, 3, 5, 6, 7))
+
+    def layer(h):
+        for b in range(4):
+            mm(banks[h][b], "qw", "sw", 128 * b, "qz", "sz", HC * h, HC * h + HC)
+        mm(banks[h][4], "qup", "sup", 128, "qz", "sz", HC * h, HC * h + HC)
+
+    def evac(h, b, q):
+        scaled(q, a("hl", 4 * HC * h + b, 4 * HC * (h + 1), 4), bank(banks[h][b], 0, HC), 0.03125)
+
+    def signs(h):
+        act(a("sgn", 80 * h, 80 * h + 80), bank(banks[h][4], 0, HC, 2), AF.Sign)
+
+    def steps(h):
+        lo, hi = HC * h, HC * h + HC
+        tt(a("f1", 80 * h, 80 * h + 80), a("sgn", 80 * h, 80 * h + 80), a("lb3", lo, hi, 2), A.add)
+        tt(a("f2", 80 * h, 80 * h + 80), a("f1", 80 * h, 80 * h + 80), a("lb3", C + lo, C + hi, 2), A.min)
+        tt(a("lb3", lo, hi, 2), a("f2", 80 * h, 80 * h + 80), a("lb3", 2 * C + lo, 2 * C + hi, 2), A.max)
+
+    def finish(h):
+        lo, hi = HC * h, HC * h + HC
+        quant("qh", "sh", lo, hi, a("hl", 4 * lo, 4 * hi))
+        mm(banks[h][5], "qv", "sv", 0, "qh", "sh", lo, hi)
+        store("y", T.oc[:, 4 * lo:4 * hi], T.qh[:, lo:hi].bitcast(dt.uint8), a("qh", lo, hi))
+
+    def result(h):
+        lo, hi = HC * h, HC * h + HC
+        act(a("ysb", lo, hi), bank(banks[h][5], 0, HC), AF.Copy)
+        store("s", T.y[:, lo:hi], T.ysb[:, lo:hi], a("ysb", lo, hi))
+
+    reading(2, order, 0, HC)
+    layer(0)
+    for b in range(4):
+        evac(0, b, "s")
+    signs(0)
+    reading(2, order, HC, C)
+    layer(1)
+    finish(0)
+    evac(1, 0, "s")
+    evac(1, 1, "v")
+    evac(1, 2, "s")
+    evac(1, 3, "v")
+    signs(1)
+    finish(1)
+    for k in range(4):
+        store("y", T.osc[4 * k:4 * k + 4, :], T.sh[32 * k:32 * k + 4, :], a("sh"))
+    result(0)
+    steps(0)
+    result(1)
+    steps(1)
+    store("y", T.ol[:], T.lb3[0:128:16, 0:C], a("lb3", 0, C))
+    total = schedule(ops, queues, T)
+    Y.wait_ge(T.sem.dout, total["dout"])
+    g.wait_ge(T.sem.snt, total["snt"])

@@ -2,29 +2,30 @@ from concourse.mybir import dt, AluOpType, ActivationFunctionType
 
 C, B, R = 320, 96, 3
 LV = 4 * C
-HC = C // 2
+HC = 192
 BIG = 1.0e29
-SP = (19, 18, 17, 16, 15)
+SP = (19, 18, 17, 16, 13)
+NEG = 12
 F8 = "float8_e4m3fn_x4"
 TILES = [(0, 320, (0, 19, 18, 17)), (1280, 256, (16, 15, 14, 13)), (2304, 192, (12, 11, 10, 9)),
          (3072, 128, (8, 7, 6, 5)), (3584, 128, (4, 3, 2, 1))]
 WIDTHS = {
-    "bfloat16": dict(ring=6 * LV, xb=16 * B, bord=24 * B, ownh=LV, z=LV, hl=LV, gt=512, ub=512, vb=512, eb=520, ob=512,
+    "bfloat16": dict(ring=6 * LV, xb=12 * B, bord=24 * B, ownh=LV, z=LV, hl=LV, gt=512, ub=512, vb=512, eb=520, ob=1024,
                      ct=4096, sgn2=20 * C, m16=16, d128=128, c16=128, tab=16, m01=C, keep=C, msg=C, dbb=C, mpp=C, spp=C,
-                     seg=C, sgn=C, ml=C, sl=C),
-    F8: dict(qx=4 * B, lq=6 * B, qz=C, qh=C, qg=256, qu=128, qup=256, qv=128, qw=512, qe=640, qc=1024),
-    "uint8": dict(sx=4 * B, ls=6 * B, sz=C, sh=C, sg=256, su=128, sup=256, sv=128, sw=512, se=640, sc=1024),
-    "float32": dict(rs=20, pf=8, r16=16, i4=C, k16=20, r4=B, tabl=50, mbig=C, kk=C, m4=B, keep4=B, base=20, lf=80, a44=40,
+                     seg=C, sgn=C, ml=C, sl=C, kk=C, m2=C, o2=C),
+    F8: dict(qx=4 * B, lq=6 * B, qz=C, qh=C, qg=256, qu=128, qup=256, qv=128, qw=512, qe=768, qc=1024),
+    "uint8": dict(sx=4 * B, ls=6 * B, sz=C, sh=C, sg=256, su=128, sup=256, sv=128, sw=512, se=768, sc=1024),
+    "float32": dict(rs=20, pf=8, r16=16, i4=C, k16=20, r4=B, tabl=50, mbig=C, m4=B, keep4=B, base=20, lf=80, a44=40,
                     dl=60, ds=20, ph=40, cb=C, mc=C, oc4=C, pa=80, pb=40, pc=80, sm=20, hlo=40, hla=40, mp=C, oh=C,
-                    t1=20, rp=20, m2=C, o2=C, rk=20, ee=C, me=B, oe=B, n1=20, n2=20, e0=20, w0=60, lm=20, l3=60,
-                    lb3=3 * C, f1=HC, f2=HC, ysb=C),
+                    t1=20, rp=20, rk=20, ee=C, me=B, oe=B, n1=20, n2=20, e0=20, w0=60, lm=20, l3=60, bs=20,
+                    lb3=3 * C, f1=C // 2, f2=C // 2, ysb=C),
     "int32": dict(pi=1, pw=8, poi=16, li=80),
     "uint16": dict(qo=20, po=16, au=20, d5=20, oo=80, fo=20, pu=80, ru=20, go=24, l3u=60),
 }
 SCRATCH = {k: ("sbuf", [128, n], d) for d, v in WIDTHS.items() for k, n in v.items()}
 SCRATCH["ps"] = ("psum", [128, 4096], "float32")
 SEMAPHORES = ["cv", "cs", "cp", "cg", "dxa", "dxb", "dli", "dxr", "du", "dw", "dv", "dout",
-              "arr0", "arr1", "arr2", "arr3", "snt"]
+              "arr0", "arr1", "arr2", "snt"]
 COUNTER = {"v": "cv", "s": "cs", "p": "cp", "g": "cg"}
 
 
@@ -99,9 +100,7 @@ def rank_program(g, core, T, topo):
     nxt = T.cores[(rank + 1) % len(T.cores)]
     prv = T.cores[(rank - 1) % len(T.cores)]
     rid, pid, _se = topo.addr(nxt)
-    out_mask = topo.mask(core, nxt)
-    n_out = len(topo.engines(core, nxt))
-    n_in = len(topo.engines(prv, core))
+    e_out, e_in = topo.engines(core, nxt), topo.engines(prv, core)
     V, S, P, Y = g.vector, g.scalar, g.tensor, g.sync
     queues = {"v": V, "s": S, "p": P, "y": Y, "g": g}
     ops = []
@@ -185,14 +184,15 @@ def rank_program(g, core, T, topo):
     def store(q, dst, view, x):
         return add(q, lambda: queues[q].dma_start(dst, view), [x], [], sem="dout")
 
-    def send(sem, name, x, lo, hi):
+    def send(sem, name, x, lo, hi, first=0, step=1):
         if name == "lq":
             dst, src = T.lq[:, lo:hi].bitcast(dt.uint8), x[0].bitcast(dt.uint8)
         else:
             dst, src = T.ls[:, lo:hi], x[0]
-        add("g", lambda: g.remote_dma(dst, src, T.sem[sem], T.sem.snt, pid, rid, out_mask), [x], [], sem="snt",
-            n=n_out, dma=False)
-        add("x", None, [], [a(name, lo, hi)], sem=sem, n=n_in)
+        mask = sum(1 << e for e in e_out[first::step])
+        add("g", lambda: g.remote_dma(dst, src, T.sem[sem], T.sem.snt, pid, rid, mask), [x], [], sem="snt",
+            n=len(e_out[first::step]), dma=False)
+        add("x", None, [], [a(name, lo, hi)], sem=sem, n=len(e_in[first::step]))
 
     def scaled(q, dst, src, c):
         if q == "v":
@@ -205,13 +205,17 @@ def rank_program(g, core, T, topo):
     Q16, GRP, ODD, T4, Q4, EVEN, SIG = [col("pf", j) for j in range(7)]
     X0 = 2 * LV
 
-    for k in range(4):
-        load("ys"[k % 2], "dxa" if k < 2 else "dxb", a("xb", 4 * B * k, 4 * B * (k + 1)), T.x[:, LV * k:LV * k + 4 * B])
-    for j, t in enumerate((T.la, T.lb, T.da, T.db)):
-        load("ys"[j % 2], "dli", a("li", 20 * j, 20 * j + 20), t[:])
+    load("y", "dxa", a("ring", X0, X0 + 512), T.x[:, 0:512])
+    load("s", "dli", a("li", 0, 20), T.la[:])
+    for k in range(1, 4):
+        load("ys"[k % 2], "dxb", a("xb", 4 * B * (k - 1), 4 * B * k), T.x[:, LV * k:LV * k + 4 * B])
+    for j, t in enumerate((T.lb, T.da, T.db)):
+        load("ys"[j % 2], "dli", a("li", 20 * j + 20, 20 * j + 40), t[:])
     load("s", "du", a("ub"), T.u[:])
-    xr = [load("y", "dxr", a("ring", X0 + LV * k + 4 * B, X0 + LV * (k + 1)), T.x[:, LV * k + 4 * B:LV * (k + 1)])
-          for k in range(4)]
+    xr = []
+    for k in range(4):
+        skip = 4 * B if k else 512
+        xr.append(load("y", "dxr", a("ring", X0 + LV * k + skip, X0 + LV * (k + 1)), T.x[:, LV * k + skip:LV * (k + 1)]))
     load("y", "dw", a("qw"), T.wc[:], after=xr, codes=True)
     load("y", "dw", a("sw"), T.ws[:])
     load("y", "dv", a("vb"), T.v[:])
@@ -239,30 +243,32 @@ def rank_program(g, core, T, topo):
     ms(a("keep", 0, C, 16), 0.0)
     for b in range(4):
         quant("qe", "se", 128 * b, 128 * b + 128, a("eb", 3 - b, 515 - b))
-    for lo, n, planes in TILES:
-        ms(a("ct", lo + 4 * 16 * planes[3], lo + 4 * n), 0.0)
     act(a("m01"), ind(a("m16"), a("qo")), AF.Copy)
     act(a("mbig"), a("m01"), AF.Identity, bias=-BIG, scale=2 * BIG)
     act(a("kk"), a("m01"), AF.Identity, bias=BIG, scale=-2 * BIG)
     act(a("msg"), a("m01"), AF.Identity, scale=SIG)
 
-    quant("qx", "sx", 0, 2 * B, a("xb", 0, 8 * B))
-    send("arr0", "lq", a("qx", 0, 2 * B), 0, 2 * B)
+    quant("qx", "sx", 0, 128, a("ring", X0, X0 + 512))
+    send("arr0", "lq", a("qx", 0, B), 0, B, 0, 2)
+    for lo, n, planes in TILES:
+        ms(a("ct", lo + 4 * 16 * planes[3], lo + 4 * n), 0.0)
     ms(a("gt", 4 * B, 512), 0.0)
     ms(col("rs", 0), 0.0)
     cp(a("po"), a("poi"))
-    ts(a("pa", 40, 60), a("k16"), Q16, A.add, EVEN, A.mult)
-    ts(a("pa", 60, 80), a("k16"), Q16, A.add, ODD, A.mult)
-    ts(a("base"), a("k16"), Q16, A.subtract, 15.0, A.add)
-    ms(a("kk", 0, C, 16), -BIG)
-    quant("qx", "sx", 2 * B, 4 * B, a("xb", 8 * B, 16 * B))
-    send("arr0", "ls", a("sx"), 0, 4 * B)
-    send("arr3", "lq", a("qx", 2 * B, 4 * B), 2 * B, 4 * B)
+    quant("qx", "sx", B, 4 * B, a("xb"))
+    send("arr0", "ls", a("sx"), 0, 4 * B, 1, 2)
+    send("arr0", "lq", a("qx", B, 4 * B), B, 4 * B)
     iota(a("c16"), [[1, 8], [0, 16]])
     iota(a("r4"), [[0, 24], [1, 4]])
     iota(a("tabl"), [[1, 10], [0, 5]], -4)
-    for k in range(4):
-        act(a("ring", X0 + LV * k, X0 + LV * k + 4 * B), a("xb", 4 * B * k, 4 * B * (k + 1)), AF.Copy)
+    for k in range(1, 4):
+        act(a("ring", X0 + LV * k, X0 + LV * k + 4 * B), a("xb", 4 * B * (k - 1), 4 * B * k), AF.Copy)
+    ts(a("pa", 40, 60), a("k16"), Q16, A.add, EVEN, A.mult)
+    ts(a("pa", 60, 80), a("k16"), Q16, A.add, ODD, A.mult)
+    ts(a("base", NEG + 1, 20), a("k16", NEG + 1, 20), Q16, A.subtract, 15.0, A.add)
+    ts(a("bs"), a("k16"), Q16, A.add, -1.0, A.mult)
+    ms(a("kk", 0, C, 16), -BIG)
+    ts(a("base", 0, NEG + 1), a("bs", 0, NEG + 1), 16.0 * NEG + 15.0, A.add)
 
     cp(a("au"), a("li", 0, 20))
     cp(a("lf"), a("li"))
@@ -304,19 +310,21 @@ def rank_program(g, core, T, topo):
     def bounds_sum():
         tt(a("sm"), ends("spp"), a("ds"), A.add)
 
-    def bounds():
+    def bound_hi():
         ts(a("hlo", 0, 20), a("sm"), 3.0 * LV, A.min)
+
+    def bound_lo():
         ts(a("hlo", 20, 40), a("sm"), 3.0 * LV, A.subtract, 0.0, A.max)
 
     def bounds_shift():
         tt(a("hla"), a("hlo"), a("a44"), A.add)
 
-    def unpack(lo, n, at, first, who, order):
+    def unpack(lo, n, at, order):
         w = max(n, 128)
         for b in order:
-            mm(first + b, "qe", "se", 128 * b, "lq", "ls", lo + n - w, lo + n)
+            mm(4 + b, "qe", "se", 128 * b, "lq", "ls", lo + n - w, lo + n)
         for b in order:
-            scaled(who[b], a("bord", 6 * B * b + at, 6 * B * b + at + n), bank(first + b, w - n, w), 0.5)
+            scaled("vsss"[b], a("bord", 6 * B * b + at, 6 * B * b + at + n), bank(4 + b, w - n, w), 0.5)
 
     def reading(r, order, lo=0, hi=C):
         for t in order:
@@ -338,15 +346,15 @@ def rank_program(g, core, T, topo):
     def compare(ks):
         for k in ks:
             if k not in SP:
-                ts(plane(k), bank(0, 0, 16 * k), score(k), A.is_lt)
+                ts(plane(k), bank(0, 0, 16 * k), score(k), A.is_lt if k > NEG else A.is_ge)
 
     def pack(m):
         lo, n, _p = TILES[m]
         quant("qc", "sc", lo // 4, lo // 4 + n, a("ct", lo, lo + 4 * n))
 
     def count(m, start, stop):
-        lo, n, _p = TILES[m]
-        mm(3, "qe", "se", 512, "qc", "sc", lo // 4, lo // 4 + n, start, stop)
+        lo, n, planes = TILES[m]
+        mm(3, "qe", "se", 512 if planes[3] > NEG else 640, "qc", "sc", lo // 4, lo // 4 + n, start, stop)
 
     delays_out()
     add("s", lambda: S.activation(T.sup[:, 0:256], T.su[:, 0:128].indirect(T.po[:, 0:16]), AF.Copy),
@@ -359,16 +367,17 @@ def rank_program(g, core, T, topo):
     for t in range(4):
         ts(a("ob", t, 512, 4), a("c16"), GRP, A.is_equal)
     bounds_sum()
-    ts(a("m4"), a("r4"), Q4, A.is_equal)
-    bounds()
-    quant("qe", "se", 512, 640, a("ob"))
+    ts(a("ob", 512, 1024), a("ob", 0, 512), -1.0, A.mult)
+    bound_hi()
+    bound_lo()
+    quant("qe", "se", 512, 768, a("ob"))
     bounds_shift()
-    act(a("keep4"), a("r4"), AF.Sign)
+    ts(a("m4"), a("r4"), Q4, A.is_equal)
     order = (0, 1, 2, 3)
     for t in order:
         own(0, t, "s")
-    unpack(0, 2 * B, 2 * B, 4, "vvvv", order)
-    unpack(2 * B, 2 * B, 4 * B, 0, "vsss", order)
+    act(a("keep4"), a("r4"), AF.Sign)
+    unpack(0, 4 * B, 2 * B, order)
     CUT = 16 * min(SP[:4])
 
     for r in range(R - 1):
@@ -380,14 +389,10 @@ def rank_program(g, core, T, topo):
             mm(4 + b, "qw", "sw", 128 * b, "qz", "sz", 0, C)
         mm(2, "qup", "sup", 128, "qz", "sz", 0, C)
         if r == 1:
-            tt(a("e0"), a("dl", 20, 40), a("dl", 0, 20), A.subtract)
-            ts(a("w0", 20, 40), a("dl", 20, 40), ODD, A.mult)
-            ts(a("w0", 0, 20), a("e0"), EVEN, A.mult)
+            partner_pick(1)
         tt(a("mp", CUT, C), bank(0, CUT, C), a("mbig", CUT, C), A.min)
         scan(a("oh", CUT, C), a("kk", CUT, C), a("mp", CUT, C), -BIG, A.min, A.max)
         tt(a("mp", 0, CUT), bank(0, 0, CUT), a("mbig", 0, CUT), A.min)
-        if r == 1:
-            tt(a("w0", 40, 60), a("w0", 0, 20), a("w0", 20, 40), A.subtract)
         scan(a("oh", 0, CUT), a("kk", 0, CUT), a("mp", 0, CUT), -BIG, A.min, A.max)
         for j in range(len(SP) + 1):
             if j < len(SP):
@@ -412,19 +417,36 @@ def rank_program(g, core, T, topo):
             count(m, j == 0, j == 4)
         for k in range(19, 0, -1):
             if k not in SP:
-                act(a("sgn2", C * k, C * k + 16 * k), plane(k), AF.Copy, acc=col("rs", k))
+                act(a("sgn2", C * k, C * k + 16 * k), plane(k), AF.Identity, scale=1.0 if k > NEG else -1.0,
+                    acc=col("rs", k))
         for b in range(4):
             scaled("s", a("ring", at + b, at + LV, 4), bank(4 + b), 0.03125)
         act(a("sgn"), bank(2), AF.Sign)
+        fill = [lambda: None] * 8
+        if r == 1:
+            partner_scan()
+            fill = [bounds_sum, bound_hi, bound_lo, bounds_shift,
+                    lambda: tt(a("e0"), a("dl", 20, 40), a("dl", 0, 20), A.subtract),
+                    lambda: ts(a("w0", 20, 40), a("dl", 20, 40), ODD, A.mult),
+                    lambda: ts(a("w0", 0, 20), a("e0"), EVEN, A.mult),
+                    lambda: tt(a("w0", 40, 60), a("w0", 0, 20), a("w0", 20, 40), A.subtract)]
         tt(a("m2"), bank(3), a("mbig"), A.min)
+        fill[0]()
         scan(a("o2"), a("kk"), a("m2"), -BIG, A.min, A.max)
         tt(a("rp"), a("t1"), a("rs"), A.subtract)
+        fill[1]()
         tt(a("rk"), ends("o2"), a("rp"), A.add)
+        fill[2]()
         cp(a("ru"), a("rk"))
+        fill[3]()
         scatter(a("ee"), a("ru"), a("i4"))
+        fill[4]()
         tt(a("me"), a("ee", 0, B), a("m4"), A.mult)
+        fill[5]()
         scan(a("oe"), a("keep4"), a("me"), 0.0, A.mult, A.add)
+        fill[6]()
         ts(a("go"), a("oe", 3, B, 4), T4, A.add)
+        fill[7]()
         h = a("ring", at, at + LV)
         act(a("gt", 2 * B, 4 * B), ind(h, a("go", 12, 24)), AF.Copy)
         cp(a("gt", 0, 2 * B), ind(h, a("go", 0, 12)))
@@ -437,66 +459,71 @@ def rank_program(g, core, T, topo):
         tt(a("n1"), old, ends("sl"), A.add if r == 0 else A.subtract)
         tt(a("n2"), a("n1"), a("hla", 0, 20), A.min)
         tt(new, a("n2"), a("hla", 20, 40), A.max)
-        tt(a("ds"), new, a("a44", 0, 20), A.subtract)
         ts(a("oo", 40, 60), new, 2.0, A.add)
-        ts(a("d5"), a("ds"), 1.0 / 256, A.mult)
+        tt(a("ds"), new, a("a44", 0, 20), A.subtract)
         ts(a("oo", 0, 20), new, 0.0, A.add)
+        ts(a("d5"), a("ds"), 1.0 / 256, A.mult)
         ts(a("oo", 60, 80), new, 3.0, A.add)
         ts(a("oo", 20, 40), new, 1.0, A.add)
-        delays_out()
-        own(r + 1, 2, "s")
-        own(r + 1, 3, "s")
-        own(r + 1, 1, "s")
-        own(r + 1, 0, "v")
         order = (0, 2, 3, 1)
-        partner_pick(r + 1)
+        own(r + 1, 2, "s")
         if r == 0:
+            own(1, 3, "s")
+            delays_out()
+            own(1, 0, "v")
+            own(1, 1, "v")
             quant("qv", "sv", 0, 128, a("vb"))
-            partner_scan()
-            bounds_sum()
-            bounds()
-            bounds_shift()
         else:
+            delays_out()
+            own(2, 3, "s")
+            own(2, 1, "s")
+            own(2, 0, "v")
             ts(a("e0"), new, ODD, A.mult)
-            partner_scan()
             tt(a("lm"), a("w0", 0, 20), a("ds"), A.subtract)
-            bounds_sum()
+            partner_pick(2)
             tt(a("l3", 0, 20), a("e0"), a("w0", 40, 60), A.add)
-            bounds()
+            partner_scan()
+            bounds_sum()
+            bound_hi()
+            bound_lo()
             tt(a("l3", 20, 40), a("hlo", 0, 20), a("lm"), A.add)
             tt(a("l3", 40, 60), a("hlo", 20, 40), a("lm"), A.add)
             ts(a("l3u"), a("l3"), 1.0 / 256, A.mult, 20.0, A.add)
-        unpack((4 + r) * B, B, (1 - r) * B, 4, "vsss", order)
+        unpack((4 + r) * B, B, (1 - r) * B, order)
 
     act(a("lb3"), ind(a("tabl"), a("l3u")), AF.Copy)
     banks = ((4, 5, 6, 7, 2, 4), (0, 1, 3, 5, 6, 7))
+    piece = ((0, HC), (HC, C))
 
     def layer(h):
+        lo, hi = piece[h]
         for b in range(4):
-            mm(banks[h][b], "qw", "sw", 128 * b, "qz", "sz", HC * h, HC * h + HC)
-        mm(banks[h][4], "qup", "sup", 128, "qz", "sz", HC * h, HC * h + HC)
+            mm(banks[h][b], "qw", "sw", 128 * b, "qz", "sz", lo, hi)
+        mm(banks[h][4], "qup", "sup", 128, "qz", "sz", lo, hi)
 
     def evac(h, b, q):
-        scaled(q, a("hl", 4 * HC * h + b, 4 * HC * (h + 1), 4), bank(banks[h][b], 0, HC), 0.03125)
+        lo, hi = piece[h]
+        scaled(q, a("hl", 4 * lo + b, 4 * hi, 4), bank(banks[h][b], 0, hi - lo), 0.03125)
 
     def signs(h):
-        act(a("sgn", 80 * h, 80 * h + 80), bank(banks[h][4], 0, HC, 2), AF.Sign)
+        lo, hi = piece[h]
+        act(a("sgn", lo // 2, hi // 2), bank(banks[h][4], 0, hi - lo, 2), AF.Sign)
 
     def steps(h):
-        lo, hi = HC * h, HC * h + HC
-        tt(a("f1", 80 * h, 80 * h + 80), a("sgn", 80 * h, 80 * h + 80), a("lb3", lo, hi, 2), A.add)
-        tt(a("f2", 80 * h, 80 * h + 80), a("f1", 80 * h, 80 * h + 80), a("lb3", C + lo, C + hi, 2), A.min)
-        tt(a("lb3", lo, hi, 2), a("f2", 80 * h, 80 * h + 80), a("lb3", 2 * C + lo, 2 * C + hi, 2), A.max)
+        lo, hi = piece[h]
+        return [lambda: tt(a("f1", lo // 2, hi // 2), a("sgn", lo // 2, hi // 2), a("lb3", lo, hi, 2), A.add),
+                lambda: tt(a("f2", lo // 2, hi // 2), a("f1", lo // 2, hi // 2), a("lb3", C + lo, C + hi, 2), A.min),
+                lambda: tt(a("lb3", lo, hi, 2), a("f2", lo // 2, hi // 2), a("lb3", 2 * C + lo, 2 * C + hi, 2), A.max)]
 
     def finish(h):
-        lo, hi = HC * h, HC * h + HC
+        lo, hi = piece[h]
         quant("qh", "sh", lo, hi, a("hl", 4 * lo, 4 * hi))
         mm(banks[h][5], "qv", "sv", 0, "qh", "sh", lo, hi)
         store("y", T.oc[:, 4 * lo:4 * hi], T.qh[:, lo:hi].bitcast(dt.uint8), a("qh", lo, hi))
 
     def result(h):
-        lo, hi = HC * h, HC * h + HC
-        act(a("ysb", lo, hi), bank(banks[h][5], 0, HC), AF.Copy)
+        lo, hi = piece[h]
+        act(a("ysb", lo, hi), bank(banks[h][5], 0, hi - lo), AF.Copy)
         store("s", T.y[:, lo:hi], T.ysb[:, lo:hi], a("ysb", lo, hi))
 
     reading(2, order, 0, HC)
@@ -516,9 +543,10 @@ def rank_program(g, core, T, topo):
     for k in range(4):
         store("y", T.osc[4 * k:4 * k + 4, :], T.sh[32 * k:32 * k + 4, :], a("sh"))
     result(0)
-    steps(0)
     result(1)
-    steps(1)
+    for one, two in zip(steps(0), steps(1)):
+        one()
+        two()
     store("y", T.ol[:], T.lb3[0:128:16, 0:C], a("lb3", 0, C))
     total = schedule(ops, queues, T)
     Y.wait_ge(T.sem.dout, total["dout"])

@@ -241,7 +241,7 @@ def rank_program(g, core, T, topo):
     ts(EVEN, ODD, -1.0, A.mult, 1.0, A.add)
     ts(SIG, ODD, -2.0 * LV, A.mult, float(LV), A.add)
     ms(a("keep", 0, C, 16), 0.0)
-    for b in range(4):
+    for b in range(2):
         quant("qe", "se", 128 * b, 128 * b + 128, a("eb", 3 - b, 515 - b))
     act(a("m01"), ind(a("m16"), a("qo")), AF.Copy)
     act(a("mbig"), a("m01"), AF.Identity, bias=-BIG, scale=2 * BIG)
@@ -250,11 +250,10 @@ def rank_program(g, core, T, topo):
 
     quant("qx", "sx", 0, 128, a("ring", X0, X0 + 512))
     send("arr0", "lq", a("qx", 0, B), 0, B, 0, 2)
+    for b in range(2, 4):
+        quant("qe", "se", 128 * b, 128 * b + 128, a("eb", 3 - b, 515 - b))
     for lo, n, planes in TILES:
         ms(a("ct", lo + 4 * 16 * planes[3], lo + 4 * n), 0.0)
-    ms(a("gt", 4 * B, 512), 0.0)
-    ms(col("rs", 0), 0.0)
-    cp(a("po"), a("poi"))
     quant("qx", "sx", B, 4 * B, a("xb"))
     send("arr0", "ls", a("sx"), 0, 4 * B, 1, 2)
     send("arr0", "lq", a("qx", B, 4 * B), B, 4 * B)
@@ -263,6 +262,9 @@ def rank_program(g, core, T, topo):
     iota(a("tabl"), [[1, 10], [0, 5]], -4)
     for k in range(1, 4):
         act(a("ring", X0 + LV * k, X0 + LV * k + 4 * B), a("xb", 4 * B * (k - 1), 4 * B * k), AF.Copy)
+    ms(a("gt", 4 * B, 512), 0.0)
+    ms(col("rs", 0), 0.0)
+    cp(a("po"), a("poi"))
     ts(a("pa", 40, 60), a("k16"), Q16, A.add, EVEN, A.mult)
     ts(a("pa", 60, 80), a("k16"), Q16, A.add, ODD, A.mult)
     ts(a("base", NEG + 1, 20), a("k16", NEG + 1, 20), Q16, A.subtract, 15.0, A.add)
@@ -326,10 +328,12 @@ def rank_program(g, core, T, topo):
         for b in order:
             scaled("vsss"[b], a("bord", 6 * B * b + at, 6 * B * b + at + n), bank(4 + b, w - n, w), 0.5)
 
-    def reading(r, order, lo=0, hi=C):
+    def far(r, order, lo, hi):
         for t in order:
             win = a("bord", 6 * B * t + (2 - r) * B, 6 * B * t + (6 - r) * B)
             tt(a("z", 4 * lo + t, 4 * hi, 4), ind(win, a("fo", lo // 16, hi // 16)), a("ownh", C * t + lo, C * t + hi), A.add)
+
+    def packz(lo, hi):
         quant("qz", "sz", lo, hi, a("z", 4 * lo, 4 * hi))
 
     place = {}
@@ -382,14 +386,17 @@ def rank_program(g, core, T, topo):
 
     for r in range(R - 1):
         at = (1 - r) * LV
-        reading(r, order)
+        far(r, order[:3], 0, C)
+        far(r, order[3:], 0, C // 2)
+        far(r, order[3:], C // 2, C)
+        packz(0, C // 2)
+        packz(C // 2, C)
         mm(0, "qup", "sup", 0, "qz", "sz", 0, C)
+        mm(2, "qup", "sup", 128, "qz", "sz", 0, C)
         mm(1, "qup", "sup", 0, "qz", "sz", 0, C)
         for b in range(4):
             mm(4 + b, "qw", "sw", 128 * b, "qz", "sz", 0, C)
-        mm(2, "qup", "sup", 128, "qz", "sz", 0, C)
-        if r == 1:
-            partner_pick(1)
+        act(a("sgn"), bank(2), AF.Sign)
         tt(a("mp", CUT, C), bank(0, CUT, C), a("mbig", CUT, C), A.min)
         scan(a("oh", CUT, C), a("kk", CUT, C), a("mp", CUT, C), -BIG, A.min, A.max)
         tt(a("mp", 0, CUT), bank(0, 0, CUT), a("mbig", 0, CUT), A.min)
@@ -421,69 +428,57 @@ def rank_program(g, core, T, topo):
                     acc=col("rs", k))
         for b in range(4):
             scaled("s", a("ring", at + b, at + LV, 4), bank(4 + b), 0.03125)
-        act(a("sgn"), bank(2), AF.Sign)
-        fill = [lambda: None] * 8
-        if r == 1:
-            partner_scan()
-            fill = [bounds_sum, bound_hi, bound_lo, bounds_shift,
-                    lambda: tt(a("e0"), a("dl", 20, 40), a("dl", 0, 20), A.subtract),
-                    lambda: ts(a("w0", 20, 40), a("dl", 20, 40), ODD, A.mult),
-                    lambda: ts(a("w0", 0, 20), a("e0"), EVEN, A.mult),
-                    lambda: tt(a("w0", 40, 60), a("w0", 0, 20), a("w0", 20, 40), A.subtract)]
+        old, new = a("dl", 20 * r, 20 * r + 20), a("dl", 20 * r + 20, 20 * r + 40)
+        tt(a("ml"), ind(a("sgn"), a("pu", 40 + 20 * r, 60 + 20 * r)), a("msg"), A.mult)
         tt(a("m2"), bank(3), a("mbig"), A.min)
-        fill[0]()
+        scan(a("sl"), a("keep"), a("ml"), 0.0, A.mult, A.add)
         scan(a("o2"), a("kk"), a("m2"), -BIG, A.min, A.max)
         tt(a("rp"), a("t1"), a("rs"), A.subtract)
-        fill[1]()
+        tt(a("n1"), old, ends("sl"), A.add if r == 0 else A.subtract)
         tt(a("rk"), ends("o2"), a("rp"), A.add)
-        fill[2]()
+        tt(a("n2"), a("n1"), a("hla", 0, 20), A.min)
         cp(a("ru"), a("rk"))
-        fill[3]()
+        tt(new, a("n2"), a("hla", 20, 40), A.max)
         scatter(a("ee"), a("ru"), a("i4"))
-        fill[4]()
+        tt(a("ds"), new, a("a44", 0, 20), A.subtract)
         tt(a("me"), a("ee", 0, B), a("m4"), A.mult)
-        fill[5]()
+        ts(a("d5"), a("ds"), 1.0 / 256, A.mult)
         scan(a("oe"), a("keep4"), a("me"), 0.0, A.mult, A.add)
-        fill[6]()
+        ts(a("oo", 40, 60), new, 2.0, A.add)
         ts(a("go"), a("oe", 3, B, 4), T4, A.add)
-        fill[7]()
+        ts(a("oo", 0, 20), new, 0.0, A.add)
         h = a("ring", at, at + LV)
         act(a("gt", 2 * B, 4 * B), ind(h, a("go", 12, 24)), AF.Copy)
         cp(a("gt", 0, 2 * B), ind(h, a("go", 0, 12)))
+        ts(a("oo", 60, 80), new, 3.0, A.add)
         quant("qg", "sg", 128 * r, 128 * r + 128, a("gt"))
         send("arr%d" % (r + 1), "lq", a("qg", 128 * r, 128 * r + B), (4 + r) * B, (5 + r) * B)
         send("arr%d" % (r + 1), "ls", a("sg", 128 * r, 128 * r + B), (4 + r) * B, (5 + r) * B)
-        tt(a("ml"), ind(a("sgn"), a("pu", 40 + 20 * r, 60 + 20 * r)), a("msg"), A.mult)
-        scan(a("sl"), a("keep"), a("ml"), 0.0, A.mult, A.add)
-        old, new = a("dl", 20 * r, 20 * r + 20), a("dl", 20 * r + 20, 20 * r + 40)
-        tt(a("n1"), old, ends("sl"), A.add if r == 0 else A.subtract)
-        tt(a("n2"), a("n1"), a("hla", 0, 20), A.min)
-        tt(new, a("n2"), a("hla", 20, 40), A.max)
-        ts(a("oo", 40, 60), new, 2.0, A.add)
-        tt(a("ds"), new, a("a44", 0, 20), A.subtract)
-        ts(a("oo", 0, 20), new, 0.0, A.add)
-        ts(a("d5"), a("ds"), 1.0 / 256, A.mult)
-        ts(a("oo", 60, 80), new, 3.0, A.add)
         ts(a("oo", 20, 40), new, 1.0, A.add)
         order = (0, 2, 3, 1)
+        delays_out()
         own(r + 1, 2, "s")
+        own(r + 1, 3, "s")
+        own(r + 1, 1, "s")
+        own(r + 1, 0, "v")
+        partner_pick(r + 1)
         if r == 0:
-            own(1, 3, "s")
-            delays_out()
-            own(1, 0, "v")
-            own(1, 1, "v")
+            tt(a("e0"), a("dl", 20, 40), a("dl", 0, 20), A.subtract)
+            partner_scan()
+            ts(a("w0", 20, 40), a("dl", 20, 40), ODD, A.mult)
+            bounds_sum()
+            ts(a("w0", 0, 20), a("e0"), EVEN, A.mult)
+            bound_hi()
+            bound_lo()
+            tt(a("w0", 40, 60), a("w0", 0, 20), a("w0", 20, 40), A.subtract)
+            bounds_shift()
             quant("qv", "sv", 0, 128, a("vb"))
         else:
-            delays_out()
-            own(2, 3, "s")
-            own(2, 1, "s")
-            own(2, 0, "v")
             ts(a("e0"), new, ODD, A.mult)
-            tt(a("lm"), a("w0", 0, 20), a("ds"), A.subtract)
-            partner_pick(2)
-            tt(a("l3", 0, 20), a("e0"), a("w0", 40, 60), A.add)
             partner_scan()
+            tt(a("lm"), a("w0", 0, 20), a("ds"), A.subtract)
             bounds_sum()
+            tt(a("l3", 0, 20), a("e0"), a("w0", 40, 60), A.add)
             bound_hi()
             bound_lo()
             tt(a("l3", 20, 40), a("hlo", 0, 20), a("lm"), A.add)
@@ -509,11 +504,14 @@ def rank_program(g, core, T, topo):
         lo, hi = piece[h]
         act(a("sgn", lo // 2, hi // 2), bank(banks[h][4], 0, hi - lo, 2), AF.Sign)
 
-    def steps(h):
+    def step(h, j):
         lo, hi = piece[h]
-        return [lambda: tt(a("f1", lo // 2, hi // 2), a("sgn", lo // 2, hi // 2), a("lb3", lo, hi, 2), A.add),
-                lambda: tt(a("f2", lo // 2, hi // 2), a("f1", lo // 2, hi // 2), a("lb3", C + lo, C + hi, 2), A.min),
-                lambda: tt(a("lb3", lo, hi, 2), a("f2", lo // 2, hi // 2), a("lb3", 2 * C + lo, 2 * C + hi, 2), A.max)]
+        if j == 0:
+            tt(a("f1", lo // 2, hi // 2), a("sgn", lo // 2, hi // 2), a("lb3", lo, hi, 2), A.add)
+        elif j == 1:
+            tt(a("f2", lo // 2, hi // 2), a("f1", lo // 2, hi // 2), a("lb3", C + lo, C + hi, 2), A.min)
+        else:
+            tt(a("lb3", lo, hi, 2), a("f2", lo // 2, hi // 2), a("lb3", 2 * C + lo, 2 * C + hi, 2), A.max)
 
     def finish(h):
         lo, hi = piece[h]
@@ -526,27 +524,33 @@ def rank_program(g, core, T, topo):
         act(a("ysb", lo, hi), bank(banks[h][5], 0, hi - lo), AF.Copy)
         store("s", T.y[:, lo:hi], T.ysb[:, lo:hi], a("ysb", lo, hi))
 
-    reading(2, order, 0, HC)
+    far(2, order, 0, HC)
+    far(2, order[:1], HC, C)
+    packz(0, HC)
     layer(0)
     for b in range(4):
         evac(0, b, "s")
     signs(0)
-    reading(2, order, HC, C)
+    far(2, order[1:], HC, C)
+    packz(HC, C)
     layer(1)
     finish(0)
+    step(0, 0)
     evac(1, 0, "s")
     evac(1, 1, "v")
     evac(1, 2, "s")
     evac(1, 3, "v")
+    step(0, 1)
     signs(1)
     finish(1)
     for k in range(4):
         store("y", T.osc[4 * k:4 * k + 4, :], T.sh[32 * k:32 * k + 4, :], a("sh"))
     result(0)
     result(1)
-    for one, two in zip(steps(0), steps(1)):
-        one()
-        two()
+    step(1, 0)
+    step(0, 2)
+    step(1, 1)
+    step(1, 2)
     store("y", T.ol[:], T.lb3[0:128:16, 0:C], a("lb3", 0, C))
     total = schedule(ops, queues, T)
     Y.wait_ge(T.sem.dout, total["dout"])

@@ -4,23 +4,24 @@ C, B, R = 320, 96, 3
 LV = 4 * C
 HC = 192
 BIG = 1.0e29
-SP = (19, 18, 17, 16, 13)
-NEG = 12
+STEP = 4096.0
+SP = (19, 18, 17, 16, 15)
+VS = (9, 10, 11, 12)
 F8 = "float8_e4m3fn_x4"
 TILES = [(0, 320, (0, 19, 18, 17)), (1280, 256, (16, 15, 14, 13)), (2304, 192, (12, 11, 10, 9)),
          (3072, 128, (8, 7, 6, 5)), (3584, 128, (4, 3, 2, 1))]
 WIDTHS = {
-    "bfloat16": dict(ring=6 * LV, xb=12 * B, bord=24 * B, ownh=LV, z=LV, hl=LV, gt=512, ub=512, vb=512, eb=520, ob=1024,
-                     ct=4096, sgn2=20 * C, m16=16, d128=128, c16=128, tab=16, m01=C, keep=C, msg=C, dbb=C, mpp=C, spp=C,
-                     seg=C, sgn=C, ml=C, sl=C, kk=C, m2=C, o2=C),
-    F8: dict(qx=4 * B, lq=6 * B, qz=C, qh=C, qg=256, qu=128, qup=256, qv=128, qw=512, qe=768, qc=1024),
-    "uint8": dict(sx=4 * B, ls=6 * B, sz=C, sh=C, sg=256, su=128, sup=256, sv=128, sw=512, se=768, sc=1024),
-    "float32": dict(rs=20, pf=8, r16=16, i4=C, k16=20, r4=B, tabl=50, mbig=C, m4=B, keep4=B, base=20, lf=80, a44=40,
-                    dl=60, ds=20, ph=40, cb=C, mc=C, oc4=C, pa=80, pb=40, pc=80, sm=20, hlo=40, hla=40, mp=C, oh=C,
-                    t1=20, rp=20, rk=20, ee=C, me=B, oe=B, n1=20, n2=20, e0=20, w0=60, lm=20, l3=60, bs=20,
-                    lb3=3 * C, f1=C // 2, f2=C // 2, ysb=C),
-    "int32": dict(pi=1, pw=8, poi=16, li=80),
-    "uint16": dict(qo=20, po=16, au=20, d5=20, oo=80, fo=20, pu=80, ru=20, go=24, l3u=60),
+    "bfloat16": dict(ring=6 * LV, xb=12 * B, bord=24 * B, ownh=LV, z=LV, hl=LV, gt=512, ub=512, vb=512, eb=520, ob=512,
+                     ct=4096, sgn2=20 * C, m16=16, d128=128, tab=16, m01=C, keep=C, dbb=C, mpp=C, spp=C,
+                     seg=C, sgn=C, ml=C, sl=C, kk=C, kl=C, k4=B, rsc=16 * max(VS) * len(VS)),
+    F8: dict(qx=4 * B, lq=6 * B, qz=C, qh=C, qg=256, qu=128, qup=256, qv=128, qw=512, qe=640, qc=1024),
+    "uint8": dict(sx=4 * B, ls=6 * B, sz=C, sh=C, sg=256, su=128, sup=256, sv=128, sw=512, se=640, sc=1024),
+    "float32": dict(rs=20, pf=24, i1=C, k16=20, r4=B, tabl=240, mbig=C, m4=B, base=20, lf=80, a4=20, a44=80, nid=20,
+                    dl=60, ds=20, ph=40, cb=C, ocl=C, pa=80, pb=40, pc=80, sm=20, hlo=40, hla=40, mp=C, oh=C, o2=C,
+                    t1=20, rp=20, rk=20, ee=C, oe=B, n1=20, n2=20, w0=100, w1=80, pof=16,
+                    sf=C, fi=20, lag=C, ysb=C),
+    "int32": dict(pi=1, pw=8, li=80),
+    "uint16": dict(qo=20, po=16, au=20, d5=20, oo=80, fo=20, pu=80, ru=20, go=24, fu=20),
 }
 SCRATCH = {k: ("sbuf", [128, n], d) for d, v in WIDTHS.items() for k, n in v.items()}
 SCRATCH["ps"] = ("psum", [128, 4096], "float32")
@@ -154,6 +155,9 @@ def rank_program(g, core, T, topo):
     def scan(o, d0, d1, init, op0, op1):
         return add("v", lambda: V.tensor_tensor_scan(o[0], d0[0], d1[0], init, op0, op1), [d0, d1], [o])
 
+    def pull(o, steps, x):
+        return scan(o, steps, x, 0.0, A.add, A.max)
+
     def quant(q, s, lo, hi, x):
         qq, ss = a(q, lo, hi), a(s, lo, hi)
         return add("v", lambda: V.quantize_mx(qq[0], ss[0], x[0]), [x], [qq, ss])
@@ -168,6 +172,9 @@ def rank_program(g, core, T, topo):
             kw["accum_out"] = acc[0]
         return add("s", lambda: S.activation(o[0], x[0], f, **kw), [x, bias, scale], [o] + ([acc] if acc else []))
 
+    def lin(o, x, scale=None, bias=None):
+        return act(o, x, AF.Identity, bias=bias, scale=scale)
+
     def mm(b, lq, ls, at, rq, rs, lo, hi, start=True, stop=True):
         o, v = bank(b, 0, hi - lo), [a(lq, at, at + 128), a(ls, at, at + 128), a(rq, lo, hi), a(rs, lo, hi)]
         return add("p", lambda: P.matmul_mx(o[0], v[0][0], v[1][0], v[2][0], v[3][0], start, stop), v, [o])
@@ -176,6 +183,9 @@ def rank_program(g, core, T, topo):
         if small:
             return add("g", lambda: g.iota(o[0], pat, base, cm, allow_small_or_imprecise_dtypes=True), [], [o])
         return add("g", lambda: g.iota(o[0], pat, base, cm), [], [o])
+
+    def keep_where(o, pat, base, cm):
+        return add("g", lambda: g.affine_select(o[0], o[0], pat, A.is_ge, 0.0, base, cm), [o], [o])
 
     def load(q, sem, o, src, after=(), codes=False):
         dst = o[0].bitcast(dt.uint8) if codes else o[0]
@@ -192,109 +202,118 @@ def rank_program(g, core, T, topo):
         mask = sum(1 << e for e in e_out[first::step])
         add("g", lambda: g.remote_dma(dst, src, T.sem[sem], T.sem.snt, pid, rid, mask), [x], [], sem="snt",
             n=len(e_out[first::step]), dma=False)
-        add("x", None, [], [a(name, lo, hi)], sem=sem, n=len(e_in[first::step]))
+        return add("x", None, [], [a(name, lo, hi)], sem=sem, n=len(e_in[first::step]))
 
     def scaled(q, dst, src, c):
         if q == "v":
             ts(dst, src, c, A.mult)
         else:
-            act(dst, src, AF.Identity, scale=c)
+            lin(dst, src, scale=c)
 
     col = lambda name, j: a(name, j, j + 1)
     ends = lambda name: a(name, 15, C, 16)
-    Q16, GRP, ODD, T4, Q4, EVEN, SIG = [col("pf", j) for j in range(7)]
+    Q16, ODD, T4, Q4, EVEN, SG0, SG1, CQ, C2, CR, C3, BQ, GO = [col("pf", j) for j in range(13)]
+    F0, F1, F2, F3, F4, F5, F6, F7 = [col("pf", j) for j in range(13, 21)]
     X0 = 2 * LV
+    I0 = -3 * STEP
 
     load("y", "dxa", a("ring", X0, X0 + 512), T.x[:, 0:512])
-    load("s", "dli", a("li", 0, 20), T.la[:])
     for k in range(1, 4):
         load("ys"[k % 2], "dxb", a("xb", 4 * B * (k - 1), 4 * B * k), T.x[:, LV * k:LV * k + 4 * B])
-    for j, t in enumerate((T.lb, T.da, T.db)):
-        load("ys"[j % 2], "dli", a("li", 20 * j + 20, 20 * j + 40), t[:])
-    load("s", "du", a("ub"), T.u[:])
-    xr = []
+    for j, t in enumerate((T.la, T.da, T.lb, T.db)):
+        at = (0, 40, 20, 60)[j]
+        load("ys"[j % 2], "dli", a("li", at, at + 20), t[:])
     for k in range(4):
         skip = 4 * B if k else 512
-        xr.append(load("y", "dxr", a("ring", X0 + LV * k + skip, X0 + LV * (k + 1)), T.x[:, LV * k + skip:LV * (k + 1)]))
-    load("y", "dw", a("qw"), T.wc[:], after=xr, codes=True)
-    load("y", "dw", a("sw"), T.ws[:])
-    load("y", "dv", a("vb"), T.v[:])
+        load("y", "dxr", a("ring", X0 + LV * k + skip, X0 + LV * (k + 1)), T.x[:, LV * k + skip:LV * (k + 1)])
+    load("y", "du", a("ub"), T.u[:])
 
     iota(a("pi"), [[0, 1]], 0, 1, small=False)
     iota(a("d128"), [[1, 128]], 0, -1)
-    iota(a("r16"), [[1, 16]])
     iota(a("k16"), [[16, 20]])
-    iota(a("poi"), [[1, 2], [16, 8]], small=False)
-    iota(a("tab"), [[256, 16]])
-    iota(a("i4"), [[4, C]])
+    iota(a("i1"), [[1, C]], int(I0))
     ms(a("eb"), 0.0)
     ts(col("pw", 0), a("pi"), 15, A.bitwise_and)
-    ts(col("pw", 1), a("pi"), 4, A.logical_shift_right)
-    ts(col("pw", 2), a("pi"), 1, A.bitwise_and)
-    ts(col("pw", 3), a("pi"), 3, A.bitwise_and)
-    ts(col("pw", 4), a("pi"), 2, A.logical_shift_right, 3, A.bitwise_and)
+    ts(col("pw", 1), a("pi"), 1, A.bitwise_and)
+    ts(col("pw", 2), a("pi"), 3, A.bitwise_and)
+    ts(col("pw", 3), a("pi"), 2, A.logical_shift_right, 3, A.bitwise_and)
     ts(a("eb", 3, 515, 4), a("d128"), 0.0, A.is_equal)
-    cp(a("pf", 0, 5), a("pw", 0, 5))
+    cp(a("pf", 0, 4), a("pw", 0, 4))
     ms(a("keep"), 1.0)
-    ts(a("m16"), a("r16"), Q16, A.is_equal)
+    ts(a("m16"), a("k16", 0, 16), 1.0 / 16, A.mult, Q16, A.is_equal)
     ts(a("qo"), a("k16"), 0.0, A.mult, Q16, A.add)
-    ts(EVEN, ODD, -1.0, A.mult, 1.0, A.add)
-    ts(SIG, ODD, -2.0 * LV, A.mult, float(LV), A.add)
-    ms(a("keep", 0, C, 16), 0.0)
     for b in range(2):
         quant("qe", "se", 128 * b, 128 * b + 128, a("eb", 3 - b, 515 - b))
+    lin(EVEN, ODD, -1.0, 1.0)
+    lin(CQ, Q16, -STEP, 15 * STEP)
+    lin(CR, Q16, -STEP, 15 * STEP + I0)
+    lin(a("nid"), a("k16"), bias=Q16)
     act(a("m01"), ind(a("m16"), a("qo")), AF.Copy)
-    act(a("mbig"), a("m01"), AF.Identity, bias=-BIG, scale=2 * BIG)
-    act(a("kk"), a("m01"), AF.Identity, bias=BIG, scale=-2 * BIG)
-    act(a("msg"), a("m01"), AF.Identity, scale=SIG)
+    lin(a("kl"), a("m01"), -BIG, STEP)
 
     quant("qx", "sx", 0, 128, a("ring", X0, X0 + 512))
     send("arr0", "lq", a("qx", 0, B), 0, B, 0, 2)
     for b in range(2, 4):
         quant("qe", "se", 128 * b, 128 * b + 128, a("eb", 3 - b, 515 - b))
-    for lo, n, planes in TILES:
-        ms(a("ct", lo + 4 * 16 * planes[3], lo + 4 * n), 0.0)
+    ms(a("keep", 0, C, 16), 0.0)
+    ms(col("rs", 0), 0.0)
     quant("qx", "sx", B, 4 * B, a("xb"))
     send("arr0", "ls", a("sx"), 0, 4 * B, 1, 2)
-    send("arr0", "lq", a("qx", B, 4 * B), B, 4 * B)
-    iota(a("c16"), [[1, 8], [0, 16]])
+    came = send("arr0", "lq", a("qx", B, 4 * B), B, 4 * B)
+    load("y", "dw", a("qw"), T.wc[:], after=[came], codes=True)
+    load("y", "dw", a("sw"), T.ws[:])
+    load("y", "dv", a("vb"), T.v[:])
+    iota(a("tab"), [[256, 16]])
+    iota(a("pof"), [[1, 2], [16, 8]])
     iota(a("r4"), [[0, 24], [1, 4]])
-    iota(a("tabl"), [[1, 10], [0, 5]], -4)
+    for lo, n, planes in TILES:
+        iota(a("ct", lo + 4 * 16 * planes[3], lo + 4 * n), [[0, 4 * n - 64 * planes[3]]])
+    iota(a("ob"), [[0, 512]], 1)
+    keep_where(a("ob"), [[-16, 8], [0, 64]], 0, 1)
+    keep_where(a("ob"), [[16, 8], [0, 64]], 15, -1)
+    iota(a("gt", 4 * B, 512), [[0, 128]])
+    iota(a("tabl"), [[1, 3], [0, 80]], -1)
+    for lag in (-1, 0, 1):
+        for d in range(3):
+            up, down = 80 * (lag + 1) + 20 * d + 7, 80 * (lag + 1) + 20 * d + 20
+            iota(a("tabl", up, up + 11, 5), [[0, 3]], lag + 1)
+            iota(a("tabl", down, down + 11, 5), [[0, 3]], lag - 1)
     for k in range(1, 4):
         act(a("ring", X0 + LV * k, X0 + LV * k + 4 * B), a("xb", 4 * B * (k - 1), 4 * B * k), AF.Copy)
-    ms(a("gt", 4 * B, 512), 0.0)
-    ms(col("rs", 0), 0.0)
-    cp(a("po"), a("poi"))
-    ts(a("pa", 40, 60), a("k16"), Q16, A.add, EVEN, A.mult)
-    ts(a("pa", 60, 80), a("k16"), Q16, A.add, ODD, A.mult)
-    ts(a("base", NEG + 1, 20), a("k16", NEG + 1, 20), Q16, A.subtract, 15.0, A.add)
-    ts(a("bs"), a("k16"), Q16, A.add, -1.0, A.mult)
-    ms(a("kk", 0, C, 16), -BIG)
-    ts(a("base", 0, NEG + 1), a("bs", 0, NEG + 1), 16.0 * NEG + 15.0, A.add)
 
+    la = a("lf", 0, 20)
     cp(a("au"), a("li", 0, 20))
     cp(a("lf"), a("li"))
-    scatter(a("cb"), a("au"), a("i4"))
-    ts(a("ds"), a("lf", 40, 60), float(LV), A.mult)
-    ts(a("a44", 0, 20), a("lf", 0, 20), 4.0, A.mult)
+    ts(a("ds"), a("li", 40, 60), float(LV), A.mult)
+    ts(a("a4"), a("li", 0, 20), 4.0, A.mult)
+    ts(a("ph", 0, 20), a("li", 60, 80), float(B), A.mult)
+    tt(a("dl", 0, 20), a("ds"), a("a4"), A.add)
     ts(a("d5"), a("ds"), 1.0 / 256, A.mult)
-    tt(a("dl", 0, 20), a("ds"), a("a44", 0, 20), A.add)
-    tt(a("mc"), a("cb"), a("m01"), A.mult)
+    tt(a("ph", 20, 40), a("ph", 0, 20), a("lf", 20, 40), A.add)
     for t in range(4):
         ts(a("oo", 20 * t, 20 * t + 20), a("dl", 0, 20), float(t), A.add)
-    scan(a("oc4"), a("keep"), a("mc"), 0.0, A.mult, A.add)
-    ts(a("pb", 0, 20), a("lf", 0, 20), ODD, A.mult)
-    ts(a("pb", 20, 40), a("lf", 0, 20), EVEN, A.mult)
-    ts(a("pa", 0, 20), ends("oc4"), 0.25, A.mult, EVEN, A.mult)
-    ts(a("pa", 20, 40), ends("oc4"), 0.25, A.mult, ODD, A.mult)
-    tt(a("pc", 40, 80), a("pa", 40, 80), a("pb"), A.add)
-    ts(a("ph", 0, 20), a("lf", 60, 80), float(B), A.mult)
-    tt(a("pc", 0, 40), a("pa", 0, 40), a("pb"), A.add)
-    tt(a("ph", 20, 40), a("ph", 0, 20), a("lf", 20, 40), A.add)
-    ts(a("a44", 20, 40), a("lf", 0, 20), 4.0, A.mult)
-    cp(a("pu"), a("pc"))
     cp(a("fo"), a("ph", 20, 40))
+    lin(a("pb", 0, 20), la, ODD)
+    lin(a("pb", 20, 40), la, EVEN)
+    lin(a("pa", 40, 60), a("nid"), EVEN)
+    lin(a("pa", 60, 80), a("nid"), ODD)
+    lin(a("mbig"), a("m01"), 2 * BIG, -BIG)
+    lin(a("kk"), a("m01"), -2 * BIG, BIG)
+    lin(C3, Q16, -STEP, 15 * STEP + 3.0 * LV)
+    lin(a("kk", 0, C, 16), a("k16"), 0.0, -BIG)
+    scatter(a("cb"), a("au"), a("i1"))
+    tt(a("pc", 40, 80), a("pa", 40, 80), a("pb"), A.add)
+    pull(a("ocl"), a("kl"), a("cb"))
+    cp(a("po"), a("pof"))
+    ts(a("pa", 0, 20), ends("ocl"), CR, A.subtract, EVEN, A.mult)
+    ts(a("pa", 20, 40), ends("ocl"), CR, A.subtract, ODD, A.mult)
+    ts(a("m4"), a("r4"), Q4, A.is_equal)
+    tt(a("pc", 0, 40), a("pa", 0, 40), a("pb"), A.add)
     quant("qu", "su", 0, 128, a("ub"))
+    cp(a("pu"), a("pc"))
+    add("v", lambda: V.tensor_copy(T.qup[:, 0:256].bitcast(dt.uint32),
+                                   T.qu[:, 0:128].bitcast(dt.uint32).indirect(T.po[:, 0:16])),
+        [a("qu"), a("po")], [a("qup")])
 
     def delays_out():
         act(a("dbb"), ind(a("tab"), a("d5")), AF.Copy)
@@ -303,30 +322,32 @@ def rank_program(g, core, T, topo):
         src = ind(a("ring", (2 - r) * LV, (6 - r) * LV), a("oo", 20 * t, 20 * t + 20))
         scaled(q, a("ownh", C * t, C * t + C), src, 0.5)
 
-    def partner_pick(r):
-        tt(a("mpp"), ind(a("dbb"), a("pu", 20 * (r % 2), 20 * (r % 2) + 20)), a("m01"), A.mult)
+    def partner_pick(r, q):
+        scaled(q, a("mpp"), ind(a("dbb"), a("pu", 20 * (r % 2), 20 * (r % 2) + 20)), 1.0)
 
     def partner_scan():
-        scan(a("spp"), a("keep"), a("mpp"), 0.0, A.mult, A.add)
+        pull(a("spp"), a("kl"), a("mpp"))
 
     def bounds_sum():
         tt(a("sm"), ends("spp"), a("ds"), A.add)
 
     def bound_hi():
-        ts(a("hlo", 0, 20), a("sm"), 3.0 * LV, A.min)
+        ts(a("hlo", 0, 20), a("sm"), CQ, A.subtract, 3.0 * LV, A.min)
 
     def bound_lo():
-        ts(a("hlo", 20, 40), a("sm"), 3.0 * LV, A.subtract, 0.0, A.max)
+        ts(a("hlo", 20, 40), a("sm"), C3, A.subtract, 0.0, A.max)
 
-    def bounds_shift():
-        tt(a("hla"), a("hlo"), a("a44"), A.add)
+    def bounds_shift(r):
+        tt(a("hla"), a("hlo"), a("a44", 40 * r, 40 * r + 40), A.add)
 
-    def unpack(lo, n, at, order):
+    def unpack(lo, n, at, order, last=None):
         w = max(n, 128)
         for b in order:
             mm(4 + b, "qe", "se", 128 * b, "lq", "ls", lo + n - w, lo + n)
         for b in order:
             scaled("vsss"[b], a("bord", 6 * B * b + at, 6 * B * b + at + n), bank(4 + b, w - n, w), 0.5)
+            if last and b == order[2]:
+                last()
 
     def far(r, order, lo, hi):
         for t in order:
@@ -350,7 +371,7 @@ def rank_program(g, core, T, topo):
     def compare(ks):
         for k in ks:
             if k not in SP:
-                ts(plane(k), bank(0, 0, 16 * k), score(k), A.is_lt if k > NEG else A.is_ge)
+                ts(plane(k), bank(0, 0, 16 * k), score(k), A.is_lt)
 
     def pack(m):
         lo, n, _p = TILES[m]
@@ -358,48 +379,71 @@ def rank_program(g, core, T, topo):
 
     def count(m, start, stop):
         lo, n, planes = TILES[m]
-        mm(3, "qe", "se", 512 if planes[3] > NEG else 640, "qc", "sc", lo // 4, lo // 4 + n, start, stop)
+        mm(3, "qe", "se", 512, "qc", "sc", lo // 4, lo // 4 + n, start, stop)
 
-    delays_out()
-    add("s", lambda: S.activation(T.sup[:, 0:256], T.su[:, 0:128].indirect(T.po[:, 0:16]), AF.Copy),
-        [a("su"), a("po")], [a("sup")])
-    partner_pick(0)
-    add("v", lambda: V.tensor_copy(T.qup[:, 0:256].bitcast(dt.uint32),
-                                   T.qu[:, 0:128].bitcast(dt.uint32).indirect(T.po[:, 0:16])),
-        [a("qu"), a("po")], [a("qup")])
-    partner_scan()
-    for t in range(4):
-        ts(a("ob", t, 512, 4), a("c16"), GRP, A.is_equal)
-    bounds_sum()
-    ts(a("ob", 512, 1024), a("ob", 0, 512), -1.0, A.mult)
-    bound_hi()
-    bound_lo()
-    quant("qe", "se", 512, 768, a("ob"))
-    bounds_shift()
-    ts(a("m4"), a("r4"), Q4, A.is_equal)
+    WS = 16 * max(VS)
+
+    def rows(k):
+        end = WS * (k - VS[0] + 1)
+        scan(a("rsc", end - 16 * k, end), plane(k), plane(k), 0.0, A.add, A.max)
+
     order = (0, 1, 2, 3)
-    for t in order:
+    for t in order[:3]:
         own(0, t, "s")
-    act(a("keep4"), a("r4"), AF.Sign)
+    own(0, 3, "v")
+    delays_out()
+
+    def picked_scales():
+        add("s", lambda: S.activation(T.sup[:, 0:256], T.su[:, 0:128].indirect(T.po[:, 0:16]), AF.Copy),
+            [a("su"), a("po")], [a("sup")])
+
     unpack(0, 4 * B, 2 * B, order)
-    CUT = 16 * min(SP[:4])
+    picked_scales()
+    CUT = 16 * min(SP + (14,))
+    w0 = lambda j: a("w0", 20 * j, 20 * j + 20)
+    w1 = lambda j: a("w1", 20 * j, 20 * j + 20)
 
     for r in range(R - 1):
         at = (1 - r) * LV
+        if r == 1:
+            delays_out()
+        partner_pick(r, "s")
+        if r == 0:
+            lin(C2, Q16, -2 * STEP, 30 * STEP)
+            lin(BQ, Q16, STEP - 1, 15 - 15 * STEP)
+        else:
+            lin(F0, ODD, 1.0 / 16, -1.0 / 16)
+            lin(F1, ODD, 1.0 / 64, -1.0 / 64)
+            lin(F2, ODD, -1.0 / 8, 1.0 / 16)
+            lin(F5, ODD, 9.0 / 256, -281.0 / 256)
+            lin(F6, ODD, 75.0, 81.0)
+            lin(F3, ODD, 3.0 / 64, 1.0 / 64)
+            lin(F4, ODD, -1.0 / 256, 1.0 / 256)
+            lin(F7, CQ, F5, F6)
+            lin(w0(1), a("a4"), F1)
+            lin(w0(2), a("dl", 20, 40), F2)
+            lin(w0(0), a("dl", 0, 20), F0, F7)
         far(r, order[:3], 0, C)
         far(r, order[3:], 0, C // 2)
         far(r, order[3:], C // 2, C)
         packz(0, C // 2)
         packz(C // 2, C)
         mm(0, "qup", "sup", 0, "qz", "sz", 0, C)
-        mm(2, "qup", "sup", 128, "qz", "sz", 0, C)
         mm(1, "qup", "sup", 0, "qz", "sz", 0, C)
+        mm(2, "qup", "sup", 128, "qz", "sz", 0, C)
         for b in range(4):
             mm(4 + b, "qw", "sw", 128 * b, "qz", "sz", 0, C)
-        act(a("sgn"), bank(2), AF.Sign)
+        partner_scan()
+        if r == 0:
+            lin(a("base"), a("k16"), bias=BQ)
+            for j in range(4):
+                lin(a("a44", 20 * j, 20 * j + 20), la, 4.0, (CQ, C2)[j // 2])
+        else:
+            quant("qv", "sv", 0, 128, a("vb"))
+        bounds_sum()
         tt(a("mp", CUT, C), bank(0, CUT, C), a("mbig", CUT, C), A.min)
-        scan(a("oh", CUT, C), a("kk", CUT, C), a("mp", CUT, C), -BIG, A.min, A.max)
         tt(a("mp", 0, CUT), bank(0, 0, CUT), a("mbig", 0, CUT), A.min)
+        scan(a("oh", CUT, C), a("kk", CUT, C), a("mp", CUT, C), -BIG, A.min, A.max)
         scan(a("oh", 0, CUT), a("kk", 0, CUT), a("mp", 0, CUT), -BIG, A.min, A.max)
         for j in range(len(SP) + 1):
             if j < len(SP):
@@ -412,89 +456,93 @@ def rank_program(g, core, T, topo):
         tt(plane(0), a("oh"), bank(0), A.is_ge)
         compare((12, 11, 10, 9))
         scan(a("seg"), a("keep"), plane(0), 0.0, A.mult, A.add)
-        pack(0)
-        compare((8, 7, 6, 5))
+        if r == 0:
+            quant("qe", "se", 512, 640, a("ob"))
         pack(2)
+        compare((8, 7, 6, 5))
         tt(a("t1"), a("base"), ends("seg"), A.subtract)
         compare((4, 3, 2, 1))
-        pack(1)
+        pack(0)
         pack(3)
         pack(4)
-        for j, m in enumerate((0, 2, 1, 3, 4)):
+        pack(1)
+        for j, m in enumerate((0, 2, 3, 4, 1)):
             count(m, j == 0, j == 4)
         for k in range(19, 0, -1):
-            if k not in SP:
-                act(a("sgn2", C * k, C * k + 16 * k), plane(k), AF.Identity, scale=1.0 if k > NEG else -1.0,
-                    acc=col("rs", k))
+            if k not in SP and k not in VS:
+                act(a("sgn2", C * k, C * k + 16 * k), plane(k), AF.Identity, acc=col("rs", k))
+        act(a("sgn"), bank(2), AF.Sign)
+        if r == 0:
+            lin(SG0, ODD, -2.0 * LV, float(LV))
+            lin(SG1, ODD, 2.0 * LV, -float(LV))
+            lin(GO, Q4, 4 * STEP, T4)
+            lin(a("k4"), a("m4"), -BIG, STEP)
+        lin(a("ml"), ind(a("sgn"), a("pu", 40 + 20 * r, 60 + 20 * r)), (SG0, SG1)[r])
         for b in range(4):
             scaled("s", a("ring", at + b, at + LV, 4), bank(4 + b), 0.03125)
         old, new = a("dl", 20 * r, 20 * r + 20), a("dl", 20 * r + 20, 20 * r + 40)
-        tt(a("ml"), ind(a("sgn"), a("pu", 40 + 20 * r, 60 + 20 * r)), a("msg"), A.mult)
-        tt(a("m2"), bank(3), a("mbig"), A.min)
-        scan(a("sl"), a("keep"), a("ml"), 0.0, A.mult, A.add)
-        scan(a("o2"), a("kk"), a("m2"), -BIG, A.min, A.max)
+        shift = (CQ, C2)[r]
+        for k in VS:
+            rows(k)
+        bound_hi()
+        cp(a("rs", VS[0], VS[-1] + 1), a("rsc", WS - 1, WS * len(VS), WS))
+        pull(a("o2"), a("kl"), bank(3))
         tt(a("rp"), a("t1"), a("rs"), A.subtract)
-        tt(a("n1"), old, ends("sl"), A.add if r == 0 else A.subtract)
+        bound_lo()
         tt(a("rk"), ends("o2"), a("rp"), A.add)
-        tt(a("n2"), a("n1"), a("hla", 0, 20), A.min)
+        bounds_shift(r)
         cp(a("ru"), a("rk"))
-        tt(new, a("n2"), a("hla", 20, 40), A.max)
-        scatter(a("ee"), a("ru"), a("i4"))
-        tt(a("ds"), new, a("a44", 0, 20), A.subtract)
-        tt(a("me"), a("ee", 0, B), a("m4"), A.mult)
-        ts(a("d5"), a("ds"), 1.0 / 256, A.mult)
-        scan(a("oe"), a("keep4"), a("me"), 0.0, A.mult, A.add)
-        ts(a("oo", 40, 60), new, 2.0, A.add)
-        ts(a("go"), a("oe", 3, B, 4), T4, A.add)
-        ts(a("oo", 0, 20), new, 0.0, A.add)
+        if r == 1:
+            tt(w1(0), w0(0), w0(1), A.add)
+        scatter(a("ee"), a("ru"), a("i1"))
+        pull(a("sl"), a("kl"), a("ml"))
+        pull(a("oe"), a("k4"), a("ee", 0, B))
+        tt(a("n1"), old, ends("sl"), A.add)
+        if r == 1:
+            tt(w1(1), w1(0), w0(2), A.add)
+        ts(a("go"), a("oe", 3, B, 4), 4.0, A.mult, GO, A.add)
+        tt(a("n2"), a("n1"), a("hla", 0, 20), A.min)
         h = a("ring", at, at + LV)
         act(a("gt", 2 * B, 4 * B), ind(h, a("go", 12, 24)), AF.Copy)
         cp(a("gt", 0, 2 * B), ind(h, a("go", 0, 12)))
-        ts(a("oo", 60, 80), new, 3.0, A.add)
+        tt(new, a("n2"), a("hla", 20, 40), A.max)
         quant("qg", "sg", 128 * r, 128 * r + 128, a("gt"))
         send("arr%d" % (r + 1), "lq", a("qg", 128 * r, 128 * r + B), (4 + r) * B, (5 + r) * B)
         send("arr%d" % (r + 1), "ls", a("sg", 128 * r, 128 * r + B), (4 + r) * B, (5 + r) * B)
-        ts(a("oo", 20, 40), new, 1.0, A.add)
-        order = (0, 2, 3, 1)
-        delays_out()
-        own(r + 1, 2, "s")
-        own(r + 1, 3, "s")
-        own(r + 1, 1, "s")
-        own(r + 1, 0, "v")
-        partner_pick(r + 1)
+        offs = lambda t: ts(a("oo", 20 * t, 20 * t + 20), new, shift, A.subtract, float(t), A.add)
         if r == 0:
-            tt(a("e0"), a("dl", 20, 40), a("dl", 0, 20), A.subtract)
-            partner_scan()
-            ts(a("w0", 20, 40), a("dl", 20, 40), ODD, A.mult)
-            bounds_sum()
-            ts(a("w0", 0, 20), a("e0"), EVEN, A.mult)
-            bound_hi()
-            bound_lo()
-            tt(a("w0", 40, 60), a("w0", 0, 20), a("w0", 20, 40), A.subtract)
-            bounds_shift()
-            quant("qv", "sv", 0, 128, a("vb"))
+            offs(2)
+        tt(a("ds"), new, a("a44", 40 * r, 40 * r + 20), A.subtract)
+        offs(0)
+        offs(1)
+        ts(a("d5"), a("ds"), 1.0 / 256, A.mult)
+        if r == 1:
+            offs(2)
+        offs(3)
+        order = (0, 1, 2, 3)
+        if r == 1:
+            delays_out()
+            lin(w0(3), a("dl", 40, 60), F3)
+            partner_pick(2, "s")
+        own(r + 1, 0, "v")
+        own(r + 1, 2, "s")
+        own(r + 1, 1, "v")
+        if r == 0:
+            own(r + 1, 3, "s")
+            unpack((4 + r) * B, B, (1 - r) * B, order)
         else:
-            ts(a("e0"), new, ODD, A.mult)
             partner_scan()
-            tt(a("lm"), a("w0", 0, 20), a("ds"), A.subtract)
-            bounds_sum()
-            tt(a("l3", 0, 20), a("e0"), a("w0", 40, 60), A.add)
-            bound_hi()
-            bound_lo()
-            tt(a("l3", 20, 40), a("hlo", 0, 20), a("lm"), A.add)
-            tt(a("l3", 40, 60), a("hlo", 20, 40), a("lm"), A.add)
-            ts(a("l3u"), a("l3"), 1.0 / 256, A.mult, 20.0, A.add)
-        unpack((4 + r) * B, B, (1 - r) * B, order)
+            unpack((4 + r) * B, B, (1 - r) * B, order, lambda: own(2, 3, "s"))
+            lin(w0(4), ends("spp"), F4)
 
-    act(a("lb3"), ind(a("tabl"), a("l3u")), AF.Copy)
-    banks = ((4, 5, 6, 7, 2, 4), (0, 1, 3, 5, 6, 7))
+    banks = ((4, 5, 6, 7, 2, 5), (0, 1, 3, 4, 2, 6))
     piece = ((0, HC), (HC, C))
 
     def layer(h):
         lo, hi = piece[h]
-        for b in range(4):
-            mm(banks[h][b], "qw", "sw", 128 * b, "qz", "sz", lo, hi)
         mm(banks[h][4], "qup", "sup", 128, "qz", "sz", lo, hi)
+        for b in (1, 0, 3, 2) if h else range(4):
+            mm(banks[h][b], "qw", "sw", 128 * b, "qz", "sz", lo, hi)
 
     def evac(h, b, q):
         lo, hi = piece[h]
@@ -502,16 +550,18 @@ def rank_program(g, core, T, topo):
 
     def signs(h):
         lo, hi = piece[h]
-        act(a("sgn", lo // 2, hi // 2), bank(banks[h][4], 0, hi - lo, 2), AF.Sign)
+        act(a("sgn", lo, hi), bank(banks[h][4], 0, hi - lo), AF.Sign)
 
     def step(h, j):
         lo, hi = piece[h]
         if j == 0:
-            tt(a("f1", lo // 2, hi // 2), a("sgn", lo // 2, hi // 2), a("lb3", lo, hi, 2), A.add)
+            pull(a("sf", lo, hi), a("kl", lo, hi), a("sgn", lo, hi))
         elif j == 1:
-            tt(a("f2", lo // 2, hi // 2), a("f1", lo // 2, hi // 2), a("lb3", C + lo, C + hi, 2), A.min)
+            tt(a("fi", lo // 16, hi // 16), a("sf", lo + 15, hi, 16), a("w1", 60 + lo // 16, 60 + hi // 16), A.add)
+        elif j == 2:
+            cp(a("fu", lo // 16, hi // 16), a("fi", lo // 16, hi // 16))
         else:
-            tt(a("lb3", lo, hi, 2), a("f2", lo // 2, hi // 2), a("lb3", 2 * C + lo, 2 * C + hi, 2), A.max)
+            scaled("sv"[h], a("lag", lo, hi), ind(a("tabl"), a("fu", lo // 16, hi // 16)), 1.0)
 
     def finish(h):
         lo, hi = piece[h]
@@ -522,36 +572,40 @@ def rank_program(g, core, T, topo):
     def result(h):
         lo, hi = piece[h]
         act(a("ysb", lo, hi), bank(banks[h][5], 0, hi - lo), AF.Copy)
+        if h == 0:
+            step(0, 3)
         store("s", T.y[:, lo:hi], T.ysb[:, lo:hi], a("ysb", lo, hi))
 
     far(2, order, 0, HC)
-    far(2, order[:1], HC, C)
+    tt(w1(2), w1(1), w0(3), A.add)
     packz(0, HC)
     layer(0)
+    signs(0)
     for b in range(4):
         evac(0, b, "s")
-    signs(0)
-    far(2, order[1:], HC, C)
+    far(2, order, HC, C)
+    tt(w1(3), w1(2), w0(4), A.add)
     packz(HC, C)
     layer(1)
-    finish(0)
     step(0, 0)
+    finish(0)
+    signs(1)
     evac(1, 0, "s")
     evac(1, 1, "v")
+    step(0, 1)
     evac(1, 2, "s")
     evac(1, 3, "v")
-    step(0, 1)
-    signs(1)
+    step(0, 2)
+    step(1, 0)
     finish(1)
     for k in range(4):
         store("y", T.osc[4 * k:4 * k + 4, :], T.sh[32 * k:32 * k + 4, :], a("sh"))
-    result(0)
-    result(1)
-    step(1, 0)
-    step(0, 2)
     step(1, 1)
+    result(0)
     step(1, 2)
-    store("y", T.ol[:], T.lb3[0:128:16, 0:C], a("lb3", 0, C))
+    result(1)
+    step(1, 3)
+    store("y", T.ol[:], T.lag[0:128:16, 0:C], a("lag"))
     total = schedule(ops, queues, T)
     Y.wait_ge(T.sem.dout, total["dout"])
     g.wait_ge(T.sem.snt, total["snt"])

@@ -5,28 +5,28 @@ LV = 4 * C
 HC = 192
 BIG = 1.0e29
 STEP = 4096.0
-SP = (19, 18, 17, 16, 15)
+SP = (19, 18, 17, 16)
 VS = (9, 10, 11, 12)
+CUT = 16 * 14
 F8 = "float8_e4m3fn_x4"
 TILES = [(0, 320, (0, 19, 18, 17)), (1280, 256, (16, 15, 14, 13)), (2304, 192, (12, 11, 10, 9)),
          (3072, 128, (8, 7, 6, 5)), (3584, 128, (4, 3, 2, 1))]
 WIDTHS = {
-    "bfloat16": dict(ring=6 * LV, xb=12 * B, bord=24 * B, ownh=LV, z=LV, hl=LV, gt=512, ub=512, vb=512, eb=520, ob=512,
+    "bfloat16": dict(ring=6 * LV, bord=24 * B, hp=LV, ownh=LV, z=LV, hl=LV, ub=512, vb=512, eb=520, ob=512,
                      ct=4096, sgn2=20 * C, m16=16, d128=128, tab=16, m01=C, keep=C, dbb=C, mpp=C, spp=C,
-                     seg=C, sgn=C, ml=C, sl=C, kk=C, kl=C, k4=B, rsc=16 * max(VS) * len(VS)),
-    F8: dict(qx=4 * B, lq=6 * B, qz=C, qh=C, qg=256, qu=128, qup=256, qv=128, qw=512, qe=640, qc=1024),
-    "uint8": dict(sx=4 * B, ls=6 * B, sz=C, sh=C, sg=256, su=128, sup=256, sv=128, sw=512, se=640, sc=1024),
-    "float32": dict(rs=20, pf=24, i1=C, k16=20, r4=B, tabl=240, mbig=C, m4=B, base=20, lf=80, a4=20, a44=80, nid=20,
-                    dl=60, ds=20, ph=40, cb=C, ocl=C, pa=80, pb=40, pc=80, sm=20, hlo=40, hla=40, mp=C, oh=C, o2=C,
-                    t1=20, rp=20, rk=20, ee=C, oe=B, n1=20, n2=20, w0=100, w1=80, pof=16,
-                    sf=C, fi=20, lag=C, ysb=C),
+                     seg=C, sgn=C, ml=C, sl=C, kk=C, kl=C, rsc=16 * max(VS) * len(VS)),
+    F8: dict(qx=4 * B + 32, lq=4 * B + 2 * C, qs=2 * C, qz=C, qh=C, qu=128, qup=256, qv=128, qw=512, qe=640, qc=1024),
+    "uint8": dict(sx=4 * B + 32, ls=4 * B + 2 * C, ss=2 * C, sz=C, sh=C, su=128, sup=256, sv=128, sw=512, se=640, sc=1024),
+    "float32": dict(rs=20, pf=24, i1=C, k16=20, tabl=240, mbig=C, base=20, lf=20, a4=20, a44=80, nid=20,
+                    dl=20, dn=80, cc=80, ds=20, ph=40, cb=C, ocl=C, pa=80, pb=40, pc=80, sm=20, hlo=40, mp=C, oh=C, o2=C,
+                    t1=20, rp=20, rk=20, ee=C, oe=B, w0=100, w1=80, pof=16, sf=C, fi=20, lag=C, ysb=C),
     "int32": dict(pi=1, pw=8, li=80),
-    "uint16": dict(qo=20, po=16, au=20, d5=20, oo=80, fo=20, pu=80, ru=20, go=24, fu=20),
+    "uint16": dict(qo=20, po=16, au=20, d5=20, oo=80, fo=20, pu=80, ru=20, go=16, gin=16, fu=20),
 }
 SCRATCH = {k: ("sbuf", [128, n], d) for d, v in WIDTHS.items() for k, n in v.items()}
 SCRATCH["ps"] = ("psum", [128, 4096], "float32")
-SEMAPHORES = ["cv", "cs", "cp", "cg", "dxa", "dxb", "dli", "dxr", "du", "dw", "dv", "dout",
-              "arr0", "arr1", "arr2", "snt"]
+SEMAPHORES = ["cv", "cs", "cp", "cg", "dx0", "dx1", "dx2", "dlb", "dli", "dxr", "du", "dw", "dv", "dout",
+              "arr0", "arr1", "arr2", "lst1", "lst2", "snt"]
 COUNTER = {"v": "cv", "s": "cs", "p": "cp", "g": "cg"}
 
 
@@ -198,7 +198,7 @@ def rank_program(g, core, T, topo):
         if name == "lq":
             dst, src = T.lq[:, lo:hi].bitcast(dt.uint8), x[0].bitcast(dt.uint8)
         else:
-            dst, src = T.ls[:, lo:hi], x[0]
+            dst, src = T[name][:, lo:hi], x[0]
         mask = sum(1 << e for e in e_out[first::step])
         add("g", lambda: g.remote_dma(dst, src, T.sem[sem], T.sem.snt, pid, rid, mask), [x], [], sem="snt",
             n=len(e_out[first::step]), dma=False)
@@ -212,108 +212,115 @@ def rank_program(g, core, T, topo):
 
     col = lambda name, j: a(name, j, j + 1)
     ends = lambda name: a(name, 15, C, 16)
-    Q16, ODD, T4, Q4, EVEN, SG0, SG1, CQ, C2, CR, C3, BQ, GO = [col("pf", j) for j in range(13)]
-    F0, F1, F2, F3, F4, F5, F6, F7 = [col("pf", j) for j in range(13, 21)]
+    Q16, ODD, EVEN, SG0, SG1, CQ, C2, C3, BQ = [col("pf", j) for j in range(9)]
+    F0, F1, F2, F3, F4, F5, F6, F7 = [col("pf", j) for j in range(9, 17)]
+    w0 = lambda j: a("w0", 20 * j, 20 * j + 20)
+    w1 = lambda j: a("w1", 20 * j, 20 * j + 20)
     X0 = 2 * LV
-    I0 = -3 * STEP
 
-    load("y", "dxa", a("ring", X0, X0 + 512), T.x[:, 0:512])
-    for k in range(1, 4):
-        load("ys"[k % 2], "dxb", a("xb", 4 * B * (k - 1), 4 * B * k), T.x[:, LV * k:LV * k + 4 * B])
+    def load_x(q, sem, lo, hi):
+        load(q, sem, a("ring", X0 + lo, X0 + hi), T.x[:, lo:hi])
+
+    load_x("y", "dx0", 0, 512)
+    load_x("s", "dx1", LV, LV + 512)
+    load_x("y", "dx2", 2 * LV, 3 * LV + 512)
     for j, t in enumerate((T.la, T.da, T.lb, T.db)):
         at = (0, 40, 20, 60)[j]
-        load("ys"[j % 2], "dli", a("li", at, at + 20), t[:])
-    for k in range(4):
-        skip = 4 * B if k else 512
-        load("y", "dxr", a("ring", X0 + LV * k + skip, X0 + LV * (k + 1)), T.x[:, LV * k + skip:LV * (k + 1)])
+        load("s", ("dli", "dlb")[j // 2], a("li", at, at + 20), t[:])
+    for k in (0, 1, 3):
+        load_x("y", "dxr", LV * k + 512, LV * (k + 1))
     load("y", "du", a("ub"), T.u[:])
 
     iota(a("pi"), [[0, 1]], 0, 1, small=False)
     iota(a("d128"), [[1, 128]], 0, -1)
     iota(a("k16"), [[16, 20]])
-    iota(a("i1"), [[1, C]], int(I0))
+    iota(a("i1"), [[1, C]])
     ms(a("eb"), 0.0)
     ts(col("pw", 0), a("pi"), 15, A.bitwise_and)
     ts(col("pw", 1), a("pi"), 1, A.bitwise_and)
-    ts(col("pw", 2), a("pi"), 3, A.bitwise_and)
-    ts(col("pw", 3), a("pi"), 2, A.logical_shift_right, 3, A.bitwise_and)
-    ts(a("eb", 3, 515, 4), a("d128"), 0.0, A.is_equal)
-    cp(a("pf", 0, 4), a("pw", 0, 4))
     ms(a("keep"), 1.0)
+    cp(a("pf", 0, 2), a("pw", 0, 2))
+    ts(a("eb", 3, 515, 4), a("d128"), 0.0, A.is_equal)
+    ms(a("keep", 0, C, 16), 0.0)
     ts(a("m16"), a("k16", 0, 16), 1.0 / 16, A.mult, Q16, A.is_equal)
     ts(a("qo"), a("k16"), 0.0, A.mult, Q16, A.add)
-    for b in range(2):
-        quant("qe", "se", 128 * b, 128 * b + 128, a("eb", 3 - b, 515 - b))
     lin(EVEN, ODD, -1.0, 1.0)
     lin(CQ, Q16, -STEP, 15 * STEP)
-    lin(CR, Q16, -STEP, 15 * STEP + I0)
     lin(a("nid"), a("k16"), bias=Q16)
     act(a("m01"), ind(a("m16"), a("qo")), AF.Copy)
+    lin(BQ, Q16, STEP - 1, 15 - 15 * STEP)
+    lin(C2, Q16, -2 * STEP, 30 * STEP)
     lin(a("kl"), a("m01"), -BIG, STEP)
+    lin(a("mbig"), a("m01"), 2 * BIG, -BIG)
+    lin(C3, Q16, -STEP, 15 * STEP + 3.0 * LV)
+    lin(col("rs", 0), Q16, 0.0)
+    lin(a("base"), a("k16"), bias=BQ)
+    lin(a("cc", 0, 40, 2), a("k16"), 0.0, -BIG)
 
-    quant("qx", "sx", 0, 128, a("ring", X0, X0 + 512))
-    send("arr0", "lq", a("qx", 0, B), 0, B, 0, 2)
-    for b in range(2, 4):
-        quant("qe", "se", 128 * b, 128 * b + 128, a("eb", 3 - b, 515 - b))
-    ms(a("keep", 0, C, 16), 0.0)
-    ms(col("rs", 0), 0.0)
-    quant("qx", "sx", B, 4 * B, a("xb"))
-    send("arr0", "ls", a("sx"), 0, 4 * B, 1, 2)
+    la = a("lf")
+    quant("qe", "se", 0, 128, a("eb", 3, 515))
+    for k in range(4):
+        quant("qx", "sx", B * k, B * k + 128, a("ring", X0 + LV * k, X0 + LV * k + 512))
+        if k == 0:
+            send("arr0", "lq", a("qx", 0, B), 0, B, 0, 2)
+            iota(a("pof"), [[1, 2], [16, 8]])
+            iota(a("tab"), [[256, 16]])
+        if k < 3:
+            quant("qe", "se", 128 * k + 128, 128 * k + 256, a("eb", 2 - k, 514 - k))
+    send("arr0", "ls", a("sx", 0, 4 * B), 0, 4 * B, 1, 2)
     came = send("arr0", "lq", a("qx", B, 4 * B), B, 4 * B)
     load("y", "dw", a("qw"), T.wc[:], after=[came], codes=True)
     load("y", "dw", a("sw"), T.ws[:])
     load("y", "dv", a("vb"), T.v[:])
-    iota(a("tab"), [[256, 16]])
-    iota(a("pof"), [[1, 2], [16, 8]])
-    iota(a("r4"), [[0, 24], [1, 4]])
-    for lo, n, planes in TILES:
-        iota(a("ct", lo + 4 * 16 * planes[3], lo + 4 * n), [[0, 4 * n - 64 * planes[3]]])
     iota(a("ob"), [[0, 512]], 1)
     keep_where(a("ob"), [[-16, 8], [0, 64]], 0, 1)
     keep_where(a("ob"), [[16, 8], [0, 64]], 15, -1)
-    iota(a("gt", 4 * B, 512), [[0, 128]])
-    iota(a("tabl"), [[1, 3], [0, 80]], -1)
-    for lag in (-1, 0, 1):
-        for d in range(3):
-            up, down = 80 * (lag + 1) + 20 * d + 7, 80 * (lag + 1) + 20 * d + 20
-            iota(a("tabl", up, up + 11, 5), [[0, 3]], lag + 1)
-            iota(a("tabl", down, down + 11, 5), [[0, 3]], lag - 1)
-    for k in range(1, 4):
-        act(a("ring", X0 + LV * k, X0 + LV * k + 4 * B), a("xb", 4 * B * (k - 1), 4 * B * k), AF.Copy)
+    for lo, n, planes in TILES:
+        iota(a("ct", lo + 4 * 16 * planes[3], lo + 4 * n), [[0, 4 * n - 64 * planes[3]]])
 
-    la = a("lf", 0, 20)
-    cp(a("au"), a("li", 0, 20))
-    cp(a("lf"), a("li"))
+    def last_table():
+        iota(a("tabl"), [[1, 3], [0, 80]], -1)
+        for lag in (-1, 0, 1):
+            for d in range(3):
+                up, down = 80 * (lag + 1) + 20 * d + 7, 80 * (lag + 1) + 20 * d + 20
+                iota(a("tabl", up, up + 11, 5), [[0, 3]], lag + 1)
+                iota(a("tabl", down, down + 11, 5), [[0, 3]], lag - 1)
+
     ts(a("ds"), a("li", 40, 60), float(LV), A.mult)
     ts(a("a4"), a("li", 0, 20), 4.0, A.mult)
-    ts(a("ph", 0, 20), a("li", 60, 80), float(B), A.mult)
-    tt(a("dl", 0, 20), a("ds"), a("a4"), A.add)
+    cp(a("au"), a("li", 0, 20))
+    cp(la, a("li", 0, 20))
+    tt(a("dl"), a("ds"), a("a4"), A.add)
     ts(a("d5"), a("ds"), 1.0 / 256, A.mult)
-    tt(a("ph", 20, 40), a("ph", 0, 20), a("lf", 20, 40), A.add)
+    cp(a("po"), a("pof"))
     for t in range(4):
-        ts(a("oo", 20 * t, 20 * t + 20), a("dl", 0, 20), float(t), A.add)
-    cp(a("fo"), a("ph", 20, 40))
+        ts(a("oo", 20 * t, 20 * t + 20), a("dl"), float(t), A.add)
     lin(a("pb", 0, 20), la, ODD)
     lin(a("pb", 20, 40), la, EVEN)
     lin(a("pa", 40, 60), a("nid"), EVEN)
     lin(a("pa", 60, 80), a("nid"), ODD)
-    lin(a("mbig"), a("m01"), 2 * BIG, -BIG)
-    lin(a("kk"), a("m01"), -2 * BIG, BIG)
-    lin(C3, Q16, -STEP, 15 * STEP + 3.0 * LV)
-    lin(a("kk", 0, C, 16), a("k16"), 0.0, -BIG)
+    for j in range(4):
+        lin(a("a44", 20 * j, 20 * j + 20), la, 4.0, (CQ, C2)[j // 2])
     scatter(a("cb"), a("au"), a("i1"))
-    tt(a("pc", 40, 80), a("pa", 40, 80), a("pb"), A.add)
+    ts(a("ph", 0, 20), a("li", 60, 80), float(B), A.mult)
+    ts(a("kk"), a("keep"), 3 * BIG, A.mult, -3 * BIG, A.add)
     pull(a("ocl"), a("kl"), a("cb"))
-    cp(a("po"), a("pof"))
-    ts(a("pa", 0, 20), ends("ocl"), CR, A.subtract, EVEN, A.mult)
-    ts(a("pa", 20, 40), ends("ocl"), CR, A.subtract, ODD, A.mult)
-    ts(a("m4"), a("r4"), Q4, A.is_equal)
-    tt(a("pc", 0, 40), a("pa", 0, 40), a("pb"), A.add)
     quant("qu", "su", 0, 128, a("ub"))
-    cp(a("pu"), a("pc"))
+    ts(a("pa", 0, 20), ends("ocl"), CQ, A.subtract, EVEN, A.mult)
+    ts(a("pa", 20, 40), ends("ocl"), CQ, A.subtract, ODD, A.mult)
+    tt(a("pc", 40, 80), a("pa", 40, 80), a("pb"), A.add)
+    tt(a("pc", 0, 40), a("pa", 0, 40), a("pb"), A.add)
     add("v", lambda: V.tensor_copy(T.qup[:, 0:256].bitcast(dt.uint32),
                                    T.qu[:, 0:128].bitcast(dt.uint32).indirect(T.po[:, 0:16])),
         [a("qu"), a("po")], [a("qup")])
+    cp(a("pu"), a("pc"))
+    tt(a("ph", 20, 40), a("ph", 0, 20), a("li", 20, 40), A.add)
+    for f, scale, bias in ((F0, 1 / 16, -1 / 16), (F1, 1 / 64, -1 / 64), (F2, -1 / 8, 1 / 16), (F3, 3 / 64, 1 / 64),
+                           (F4, -1 / 256, 1 / 256), (F5, 9 / 256, -281 / 256), (F6, 75.0, 81.0),
+                           (SG0, -2.0 * LV, float(LV)), (SG1, 2.0 * LV, -float(LV))):
+        lin(f, ODD, scale, bias)
+    lin(w0(1), a("a4"), F1)
+    lin(F7, CQ, F5, F6)
 
     def delays_out():
         act(a("dbb"), ind(a("tab"), a("d5")), AF.Copy)
@@ -322,32 +329,11 @@ def rank_program(g, core, T, topo):
         src = ind(a("ring", (2 - r) * LV, (6 - r) * LV), a("oo", 20 * t, 20 * t + 20))
         scaled(q, a("ownh", C * t, C * t + C), src, 0.5)
 
-    def partner_pick(r, q):
-        scaled(q, a("mpp"), ind(a("dbb"), a("pu", 20 * (r % 2), 20 * (r % 2) + 20)), 1.0)
+    def partner_pick(r):
+        act(a("mpp"), ind(a("dbb"), a("pu", 20 * (r % 2), 20 * (r % 2) + 20)), AF.Copy)
 
     def partner_scan():
         pull(a("spp"), a("kl"), a("mpp"))
-
-    def bounds_sum():
-        tt(a("sm"), ends("spp"), a("ds"), A.add)
-
-    def bound_hi():
-        ts(a("hlo", 0, 20), a("sm"), CQ, A.subtract, 3.0 * LV, A.min)
-
-    def bound_lo():
-        ts(a("hlo", 20, 40), a("sm"), C3, A.subtract, 0.0, A.max)
-
-    def bounds_shift(r):
-        tt(a("hla"), a("hlo"), a("a44", 40 * r, 40 * r + 40), A.add)
-
-    def unpack(lo, n, at, order, last=None):
-        w = max(n, 128)
-        for b in order:
-            mm(4 + b, "qe", "se", 128 * b, "lq", "ls", lo + n - w, lo + n)
-        for b in order:
-            scaled("vsss"[b], a("bord", 6 * B * b + at, 6 * B * b + at + n), bank(4 + b, w - n, w), 0.5)
-            if last and b == order[2]:
-                last()
 
     def far(r, order, lo, hi):
         for t in order:
@@ -387,64 +373,50 @@ def rank_program(g, core, T, topo):
         end = WS * (k - VS[0] + 1)
         scan(a("rsc", end - 16 * k, end), plane(k), plane(k), 0.0, A.add, A.max)
 
-    order = (0, 1, 2, 3)
-    for t in order[:3]:
-        own(0, t, "s")
-    own(0, 3, "v")
     delays_out()
-
-    def picked_scales():
-        add("s", lambda: S.activation(T.sup[:, 0:256], T.su[:, 0:128].indirect(T.po[:, 0:16]), AF.Copy),
-            [a("su"), a("po")], [a("sup")])
-
-    unpack(0, 4 * B, 2 * B, order)
-    picked_scales()
-    CUT = 16 * min(SP + (14,))
-    w0 = lambda j: a("w0", 20 * j, 20 * j + 20)
-    w1 = lambda j: a("w1", 20 * j, 20 * j + 20)
+    lin(w0(0), a("dl"), F0, F7)
+    for t in range(4):
+        own(0, t, "s")
+    for h in range(2):
+        mm(3 + h, "qe", "se", 0, "lq", "ls", 2 * B * h, 2 * B * h + 2 * B)
+        scaled("vs"[h], a("bord", 2 * B * (h + 1), 2 * B * (h + 2)), bank(3 + h, 0, 2 * B), 0.5)
+    cp(a("fo"), a("ph", 20, 40))
+    for b in range(1, 4):
+        mm(4 + b, "qe", "se", 128 * b, "lq", "ls", 0, 4 * B)
+    for b in range(1, 4):
+        scaled("s", a("bord", 6 * B * b + 2 * B, 6 * B * (b + 1)), bank(4 + b, 0, 4 * B), 0.5)
+    add("s", lambda: S.activation(T.sup[:, 0:256], T.su[:, 0:128].indirect(T.po[:, 0:16]), AF.Copy),
+        [a("su"), a("po")], [a("sup")])
 
     for r in range(R - 1):
-        at = (1 - r) * LV
+        at, land = (1 - r) * LV, 4 * B + C * r
         if r == 1:
             delays_out()
-        partner_pick(r, "s")
-        if r == 0:
-            lin(C2, Q16, -2 * STEP, 30 * STEP)
-            lin(BQ, Q16, STEP - 1, 15 - 15 * STEP)
-        else:
-            lin(F0, ODD, 1.0 / 16, -1.0 / 16)
-            lin(F1, ODD, 1.0 / 64, -1.0 / 64)
-            lin(F2, ODD, -1.0 / 8, 1.0 / 16)
-            lin(F5, ODD, 9.0 / 256, -281.0 / 256)
-            lin(F6, ODD, 75.0, 81.0)
-            lin(F3, ODD, 3.0 / 64, 1.0 / 64)
-            lin(F4, ODD, -1.0 / 256, 1.0 / 256)
-            lin(F7, CQ, F5, F6)
-            lin(w0(1), a("a4"), F1)
-            lin(w0(2), a("dl", 20, 40), F2)
-            lin(w0(0), a("dl", 0, 20), F0, F7)
-        far(r, order[:3], 0, C)
-        far(r, order[3:], 0, C // 2)
-        far(r, order[3:], C // 2, C)
+        partner_pick(r)
+        if r == 1:
+            lin(w0(2), a("dn", 1, 40, 2), F2)
+        far(r, (0, 1, 2), 0, C)
+        far(r, (3,), 0, C // 2)
+        far(r, (3,), C // 2, C)
         packz(0, C // 2)
         packz(C // 2, C)
         mm(0, "qup", "sup", 0, "qz", "sz", 0, C)
+        for b in range(4):
+            mm(4 + b, "qw", "sw", 128 * b, "qz", "sz", 0, C)
         mm(1, "qup", "sup", 0, "qz", "sz", 0, C)
         mm(2, "qup", "sup", 128, "qz", "sz", 0, C)
         for b in range(4):
-            mm(4 + b, "qw", "sw", 128 * b, "qz", "sz", 0, C)
+            scaled("s", a("ring", at + b, at + LV, 4), bank(4 + b), 0.03125)
         partner_scan()
         if r == 0:
-            lin(a("base"), a("k16"), bias=BQ)
-            for j in range(4):
-                lin(a("a44", 20 * j, 20 * j + 20), la, 4.0, (CQ, C2)[j // 2])
+            quant("qe", "se", 512, 640, a("ob"))
         else:
             quant("qv", "sv", 0, 128, a("vb"))
-        bounds_sum()
+        tt(a("sm"), ends("spp"), a("ds"), A.add)
         tt(a("mp", CUT, C), bank(0, CUT, C), a("mbig", CUT, C), A.min)
         tt(a("mp", 0, CUT), bank(0, 0, CUT), a("mbig", 0, CUT), A.min)
-        scan(a("oh", CUT, C), a("kk", CUT, C), a("mp", CUT, C), -BIG, A.min, A.max)
-        scan(a("oh", 0, CUT), a("kk", 0, CUT), a("mp", 0, CUT), -BIG, A.min, A.max)
+        pull(a("oh", CUT, C), a("kk", CUT, C), a("mp", CUT, C))
+        pull(a("oh", 0, CUT), a("kk", 0, CUT), a("mp", 0, CUT))
         for j in range(len(SP) + 1):
             if j < len(SP):
                 k = SP[j]
@@ -454,13 +426,15 @@ def rank_program(g, core, T, topo):
                 act(plane(k), a("sgn2", C * k, C * k + 16 * k), AF.Relu, acc=col("rs", k))
         compare((19, 18, 17, 16, 15, 14, 13))
         tt(plane(0), a("oh"), bank(0), A.is_ge)
+        quant("qs", "ss", C * r, C * r + C, a("ring", at, at + LV))
+        send("arr%d" % (r + 1), "lq", a("qs", C * r, C * r + C), land, land + C)
+        send("arr%d" % (r + 1), "ls", a("ss", C * r, C * r + C), land, land + C)
+        if r == 0:
+            last_table()
         compare((12, 11, 10, 9))
         scan(a("seg"), a("keep"), plane(0), 0.0, A.mult, A.add)
-        if r == 0:
-            quant("qe", "se", 512, 640, a("ob"))
         pack(2)
         compare((8, 7, 6, 5))
-        tt(a("t1"), a("base"), ends("seg"), A.subtract)
         compare((4, 3, 2, 1))
         pack(0)
         pack(3)
@@ -472,68 +446,57 @@ def rank_program(g, core, T, topo):
             if k not in SP and k not in VS:
                 act(a("sgn2", C * k, C * k + 16 * k), plane(k), AF.Identity, acc=col("rs", k))
         act(a("sgn"), bank(2), AF.Sign)
-        if r == 0:
-            lin(SG0, ODD, -2.0 * LV, float(LV))
-            lin(SG1, ODD, 2.0 * LV, -float(LV))
-            lin(GO, Q4, 4 * STEP, T4)
-            lin(a("k4"), a("m4"), -BIG, STEP)
         lin(a("ml"), ind(a("sgn"), a("pu", 40 + 20 * r, 60 + 20 * r)), (SG0, SG1)[r])
         for b in range(4):
-            scaled("s", a("ring", at + b, at + LV, 4), bank(4 + b), 0.03125)
-        old, new = a("dl", 20 * r, 20 * r + 20), a("dl", 20 * r + 20, 20 * r + 40)
+            mm(4 + b, "qe", "se", 128 * b, "lq", "ls", land, land + C)
+        for b in range(4):
+            scaled("s", a("hp", C * b, C * b + C), bank(4 + b), 0.5)
+        old, new = (a("dl"), a("dn", 1, 40, 2))[r], a("dn", 40 * r + 1, 40 * r + 40, 2)
         shift = (CQ, C2)[r]
         for k in VS:
             rows(k)
-        bound_hi()
+        tt(a("t1"), a("base"), ends("seg"), A.subtract)
         cp(a("rs", VS[0], VS[-1] + 1), a("rsc", WS - 1, WS * len(VS), WS))
         pull(a("o2"), a("kl"), bank(3))
         tt(a("rp"), a("t1"), a("rs"), A.subtract)
-        bound_lo()
+        ts(a("hlo", 20, 40), a("sm"), C3, A.subtract, 0.0, A.max)
+        ts(a("hlo", 0, 20), a("sm"), CQ, A.subtract, 3.0 * LV, A.min)
         tt(a("rk"), ends("o2"), a("rp"), A.add)
-        bounds_shift(r)
+        tt(a("cc", 1, 80, 2), a("hlo"), a("a44", 40 * r, 40 * r + 40), A.add)
         cp(a("ru"), a("rk"))
         if r == 1:
             tt(w1(0), w0(0), w0(1), A.add)
         scatter(a("ee"), a("ru"), a("i1"))
         pull(a("sl"), a("kl"), a("ml"))
-        pull(a("oe"), a("k4"), a("ee", 0, B))
-        tt(a("n1"), old, ends("sl"), A.add)
+        pull(a("oe"), a("kl", 0, B), a("ee", 0, B))
+        tt(a("cc", 40, 80, 2), old, ends("sl"), A.add)
         if r == 1:
             tt(w1(1), w1(0), w0(2), A.add)
-        ts(a("go"), a("oe", 3, B, 4), 4.0, A.mult, GO, A.add)
-        tt(a("n2"), a("n1"), a("hla", 0, 20), A.min)
-        h = a("ring", at, at + LV)
-        act(a("gt", 2 * B, 4 * B), ind(h, a("go", 12, 24)), AF.Copy)
-        cp(a("gt", 0, 2 * B), ind(h, a("go", 0, 12)))
-        tt(new, a("n2"), a("hla", 20, 40), A.max)
-        quant("qg", "sg", 128 * r, 128 * r + 128, a("gt"))
-        send("arr%d" % (r + 1), "lq", a("qg", 128 * r, 128 * r + B), (4 + r) * B, (5 + r) * B)
-        send("arr%d" % (r + 1), "ls", a("sg", 128 * r, 128 * r + B), (4 + r) * B, (5 + r) * B)
-        offs = lambda t: ts(a("oo", 20 * t, 20 * t + 20), new, shift, A.subtract, float(t), A.add)
-        if r == 0:
-            offs(2)
-        tt(a("ds"), new, a("a44", 40 * r, 40 * r + 20), A.subtract)
-        offs(0)
+        ts(a("go", 8 * r, 8 * r + 6), a("oe", 15, B, 16), CQ, A.subtract)
+        send("lst%d" % (r + 1), "gin", a("go", 8 * r, 8 * r + 6), 8 * r, 8 * r + 6)
+        scan(a("dn", 40 * r, 40 * r + 40), a("cc", 0, 40), a("cc", 40, 80), 0.0, A.min, A.max)
+
+        def offs(t):
+            ts(a("oo", 20 * t, 20 * t + 20), new, shift, A.subtract, float(t), A.add)
+
+        def pick(t, q):
+            lo = 6 * B * t + (1 - r) * B
+            scaled(q, a("bord", lo, lo + B), ind(a("hp", C * t, C * t + C), a("gin", 8 * r, 8 * r + 6)), 1.0)
+
         offs(1)
-        ts(a("d5"), a("ds"), 1.0 / 256, A.mult)
-        if r == 1:
-            offs(2)
-        offs(3)
-        order = (0, 1, 2, 3)
-        if r == 1:
-            delays_out()
-            lin(w0(3), a("dl", 40, 60), F3)
-            partner_pick(2, "s")
+        offs(0)
+        offs(2)
         own(r + 1, 0, "v")
+        own(r + 1, 1, "s")
+        tt(a("ds"), new, a("a44", 40 * r, 40 * r + 20), A.subtract)
+        offs(3)
+        pick(0, "v")
+        ts(a("d5"), a("ds"), 1.0 / 256, A.mult)
+        pick(1, "s")
         own(r + 1, 2, "s")
-        own(r + 1, 1, "v")
-        if r == 0:
-            own(r + 1, 3, "s")
-            unpack((4 + r) * B, B, (1 - r) * B, order)
-        else:
-            partner_scan()
-            unpack((4 + r) * B, B, (1 - r) * B, order, lambda: own(2, 3, "s"))
-            lin(w0(4), ends("spp"), F4)
+        pick(2, "s")
+        own(r + 1, 3, "s")
+        pick(3, "s")
 
     banks = ((4, 5, 6, 7, 2, 5), (0, 1, 3, 4, 2, 6))
     piece = ((0, HC), (HC, C))
@@ -576,18 +539,26 @@ def rank_program(g, core, T, topo):
             step(0, 3)
         store("s", T.y[:, lo:hi], T.ysb[:, lo:hi], a("ysb", lo, hi))
 
-    far(2, order, 0, HC)
-    tt(w1(2), w1(1), w0(3), A.add)
+    delays_out()
+    partner_pick(2)
+    for t, h in ((0, 0), (1, 0), (0, 1), (2, 0), (1, 1), (3, 0)):
+        far(2, (t,), *piece[h])
+    ts(w0(3), a("dn", 41, 80, 2), F3, A.mult)
     packz(0, HC)
     layer(0)
     signs(0)
-    for b in range(4):
+    for b in range(3):
         evac(0, b, "s")
-    far(2, order, HC, C)
-    tt(w1(3), w1(2), w0(4), A.add)
+    far(2, (2,), HC, C)
+    tt(w1(2), w1(1), w0(3), A.add)
+    far(2, (3,), HC, C)
+    partner_scan()
     packz(HC, C)
     layer(1)
+    ts(w0(4), ends("spp"), F4, A.mult)
+    evac(0, 3, "v")
     step(0, 0)
+    tt(w1(3), w1(2), w0(4), A.add)
     finish(0)
     signs(1)
     evac(1, 0, "s")

from concourse.mybir import dt, AluOpType, ActivationFunctionType

C, B, R = 320, 96, 3
LV = 4 * C
HC = 192
BIG = 1.0e29
STEP = 4096.0
SP = (19, 18, 17, 16)
VS = (9, 10, 11, 12)
CUT = 16 * 14
F8 = "float8_e4m3fn_x4"
TILES = [(0, 320, (0, 19, 18, 17)), (1280, 256, (16, 15, 14, 13)), (2304, 192, (12, 11, 10, 9)),
         (3072, 128, (8, 7, 6, 5)), (3584, 128, (4, 3, 2, 1))]
WIDTHS = {
    "bfloat16": dict(ring=6 * LV, bord=24 * B, hp=LV, ownh=LV, z=LV, hl=LV, ub=512, vb=512, eb=520, ob=512,
                     ct=4096, sgn2=20 * C, m16=16, d128=128, tab=16, m01=C, keep=C, dbb=C, mpp=C, spp=C,
                     seg=C, sgn=C, ml=C, sl=C, kk=C, kl=C, rsc=16 * max(VS) * len(VS)),
    F8: dict(qx=4 * B + 32, lq=4 * B + 2 * C, qs=2 * C, qz=C, qh=C, qu=128, qup=256, qv=128, qw=512, qe=640, qc=1024),
    "uint8": dict(sx=4 * B + 32, ls=4 * B + 2 * C, ss=2 * C, sz=C, sh=C, su=128, sup=256, sv=128, sw=512, se=640, sc=1024),
    "float32": dict(rs=20, pf=24, i1=C, k16=20, tabl=240, mbig=C, base=20, lf=20, a4=20, a44=80, nid=20,
                    dl=20, dn=80, cc=80, ds=20, ph=40, cb=C, ocl=C, pa=80, pb=40, pc=80, sm=20, hlo=40, mp=C, oh=C, o2=C,
                    t1=20, rp=20, rk=20, ee=C, oe=B, w0=100, w1=80, pof=16, sf=C, fi=20, lag=C, ysb=C),
    "int32": dict(pi=1, pw=8, li=80),
    "uint16": dict(qo=20, po=16, au=20, d5=20, oo=80, fo=20, pu=80, ru=20, go=16, gin=16, fu=20),
}
SCRATCH = {k: ("sbuf", [128, n], d) for d, v in WIDTHS.items() for k, n in v.items()}
SCRATCH["ps"] = ("psum", [128, 4096], "float32")
SEMAPHORES = ["cv", "cs", "cp", "cg", "dx0", "dx1", "dx2", "dlb", "dli", "dxr", "du", "dw", "dv", "dout",
              "arr0", "arr1", "arr2", "lst1", "lst2", "snt"]
COUNTER = {"v": "cv", "s": "cs", "p": "cp", "g": "cg"}


def schedule(ops, queues, T):
    hist, known, seq, group = {}, {}, {}, {}
    for n, o in enumerate(ops):
        deps = set(o["after"])
        for acc, wr in [(a, False) for a in o["r"]] + [(a, True) for a in o["w"]]:
            name, cols = acc
            for m, c2, w2 in hist.get(name, []):
                if m == n or not (cols & c2):
                    continue
                other = ops[m]["q"] != o["q"]
                if name == "ps" and not other and o["q"] == "p":
                    continue
                if wr or w2 or (name == "ps" and other):
                    deps.add(m)
            hist.setdefault(name, []).append((n, cols, wr))
        kn = known.setdefault(o["q"], {})
        need = {}
        for m in deps:
            d = ops[m]
            key = d["sem"] or d["q"]
            lvl = 1 if d["sem"] else d["seq"]
            if kn.get(key, 0) < lvl and need.get(key, (0, 0))[0] < lvl:
                need[key] = (lvl, m)
        waits = []
        for key, (lvl, m) in sorted(need.items(), key=lambda kv: -kv[1][1]):
            if kn.get(key, 0) >= lvl:
                continue
            waits.append(m)
            ops[m]["inc"] = True
            for mm in (group[key] if ops[m]["sem"] else [m]):
                for k2, l2 in ops[mm]["clock"].items():
                    kn[k2] = max(kn.get(k2, 0), l2)
            kn[key] = lvl
        o["waits"] = waits
        o["clock"] = dict(kn)
        if o["sem"]:
            group.setdefault(o["sem"], []).append(n)
        else:
            seq[o["q"]] = seq.get(o["q"], 0) + 1
            o["seq"] = seq[o["q"]]
    count = {}
    for o in ops:
        if not o["sem"] and o["inc"]:
            count[o["q"]] = count.get(o["q"], 0) + 1
            o["count"] = count[o["q"]]
    for o in ops:
        if o["fn"] is None:
            continue
        q = queues[o["q"]]
        for m in o["waits"]:
            d = ops[m]
            if d["sem"]:
                q.wait_ge(T.sem[d["sem"]], sum(ops[k]["n"] for k in group[d["sem"]]))
            else:
                q.wait_ge(T.sem[COUNTER[d["q"]]], d["count"])
        ins = o["fn"]()
        if o["sem"] and o["dma"]:
            ins.then_inc(T.sem[o["sem"]], 16)
        elif o["inc"] and not o["sem"]:
            ins.then_inc(T.sem[COUNTER[o["q"]]], 1)
    return {k: sum(ops[m]["n"] for m in v) for k, v in group.items()}


def rank_program(g, core, T, topo):
    rank = T.rank_of(core)
    if rank is None:
        return
    A, AF = AluOpType, ActivationFunctionType
    nxt = T.cores[(rank + 1) % len(T.cores)]
    prv = T.cores[(rank - 1) % len(T.cores)]
    rid, pid, _se = topo.addr(nxt)
    e_out, e_in = topo.engines(core, nxt), topo.engines(prv, core)
    V, S, P, Y = g.vector, g.scalar, g.tensor, g.sync
    queues = {"v": V, "s": S, "p": P, "y": Y, "g": g}
    ops = []

    def a(name, lo=0, hi=None, step=1):
        if hi is None:
            hi = SCRATCH[name][1][1]
        if name == "ps":
            cols = set(range(lo // 512, (hi - 1) // 512 + 1))
        else:
            cols = set(range(lo, hi, step))
        view = T[name][:, lo:hi] if step == 1 else T[name][:, lo:hi:step]
        return (view, [(name, cols)])

    def ind(win, off):
        return (win[0].indirect(off[0]), win[1] + off[1])

    def bank(b, lo=0, hi=C, step=1):
        return a("ps", 512 * b + lo, 512 * b + hi, step)

    def add(q, fn, r=(), w=(), sem=None, n=16, dma=True, after=()):
        rr, ww = [], []
        for x in r:
            if isinstance(x, tuple):
                rr += x[1]
        for x in w:
            ww += x[1]
        ops.append({"q": q, "fn": fn, "r": rr, "w": ww, "sem": sem, "n": n, "dma": dma, "after": list(after), "inc": False})
        return len(ops) - 1

    def val(x):
        return x[0] if isinstance(x, tuple) else x

    def tt(o, x, y, op):
        return add("v", lambda: V.tensor_tensor(o[0], x[0], y[0], op), [x, y], [o])

    def ts(o, x, s1, op0, s2=None, op1=None):
        if op1 is None:
            return add("v", lambda: V.tensor_scalar(o[0], x[0], val(s1), None, op0), [x, s1], [o])
        return add("v", lambda: V.tensor_scalar(o[0], x[0], val(s1), val(s2), op0, op1), [x, s1, s2], [o])

    def cp(o, x):
        return add("v", lambda: V.tensor_copy(o[0], x[0]), [x], [o])

    def scatter(win, off, x):
        return add("v", lambda: V.tensor_copy(win[0].indirect(off[0]), x[0]), [x, off], [win])

    def ms(o, c):
        return add("v", lambda: V.memset(o[0], c), [], [o])

    def scan(o, d0, d1, init, op0, op1):
        return add("v", lambda: V.tensor_tensor_scan(o[0], d0[0], d1[0], init, op0, op1), [d0, d1], [o])

    def pull(o, steps, x):
        return scan(o, steps, x, 0.0, A.add, A.max)

    def quant(q, s, lo, hi, x):
        qq, ss = a(q, lo, hi), a(s, lo, hi)
        return add("v", lambda: V.quantize_mx(qq[0], ss[0], x[0]), [x], [qq, ss])

    def act(o, x, f, bias=None, scale=None, acc=None):
        kw = {}
        if bias is not None:
            kw["bias"] = val(bias)
        if scale is not None:
            kw["scale"] = val(scale)
        if acc is not None:
            kw["accum_out"] = acc[0]
        return add("s", lambda: S.activation(o[0], x[0], f, **kw), [x, bias, scale], [o] + ([acc] if acc else []))

    def lin(o, x, scale=None, bias=None):
        return act(o, x, AF.Identity, bias=bias, scale=scale)

    def mm(b, lq, ls, at, rq, rs, lo, hi, start=True, stop=True):
        o, v = bank(b, 0, hi - lo), [a(lq, at, at + 128), a(ls, at, at + 128), a(rq, lo, hi), a(rs, lo, hi)]
        return add("p", lambda: P.matmul_mx(o[0], v[0][0], v[1][0], v[2][0], v[3][0], start, stop), v, [o])

    def iota(o, pat, base=0, cm=0, small=True):
        if small:
            return add("g", lambda: g.iota(o[0], pat, base, cm, allow_small_or_imprecise_dtypes=True), [], [o])
        return add("g", lambda: g.iota(o[0], pat, base, cm), [], [o])

    def keep_where(o, pat, base, cm):
        return add("g", lambda: g.affine_select(o[0], o[0], pat, A.is_ge, 0.0, base, cm), [o], [o])

    def load(q, sem, o, src, after=(), codes=False):
        dst = o[0].bitcast(dt.uint8) if codes else o[0]
        return add(q, lambda: queues[q].dma_start(dst, src), [], [o], sem=sem, after=after)

    def store(q, dst, view, x):
        return add(q, lambda: queues[q].dma_start(dst, view), [x], [], sem="dout")

    def send(sem, name, x, lo, hi, first=0, step=1):
        if name == "lq":
            dst, src = T.lq[:, lo:hi].bitcast(dt.uint8), x[0].bitcast(dt.uint8)
        else:
            dst, src = T[name][:, lo:hi], x[0]
        mask = sum(1 << e for e in e_out[first::step])
        add("g", lambda: g.remote_dma(dst, src, T.sem[sem], T.sem.snt, pid, rid, mask), [x], [], sem="snt",
            n=len(e_out[first::step]), dma=False)
        return add("x", None, [], [a(name, lo, hi)], sem=sem, n=len(e_in[first::step]))

    def scaled(q, dst, src, c):
        if q == "v":
            ts(dst, src, c, A.mult)
        else:
            lin(dst, src, scale=c)

    col = lambda name, j: a(name, j, j + 1)
    ends = lambda name: a(name, 15, C, 16)
    Q16, ODD, EVEN, SG0, SG1, CQ, C2, C3, BQ = [col("pf", j) for j in range(9)]
    F0, F1, F2, F3, F4, F5, F6, F7 = [col("pf", j) for j in range(9, 17)]
    w0 = lambda j: a("w0", 20 * j, 20 * j + 20)
    w1 = lambda j: a("w1", 20 * j, 20 * j + 20)
    X0 = 2 * LV

    def load_x(q, sem, lo, hi):
        load(q, sem, a("ring", X0 + lo, X0 + hi), T.x[:, lo:hi])

    load_x("y", "dx0", 0, 512)
    load_x("s", "dx1", LV, LV + 512)
    load_x("y", "dx2", 2 * LV, 3 * LV + 512)
    for j, t in enumerate((T.la, T.da, T.lb, T.db)):
        at = (0, 40, 20, 60)[j]
        load("s", ("dli", "dlb")[j // 2], a("li", at, at + 20), t[:])
    for k in (0, 1, 3):
        load_x("y", "dxr", LV * k + 512, LV * (k + 1))
    load("y", "du", a("ub"), T.u[:])

    iota(a("pi"), [[0, 1]], 0, 1, small=False)
    iota(a("d128"), [[1, 128]], 0, -1)
    iota(a("k16"), [[16, 20]])
    iota(a("i1"), [[1, C]])
    ms(a("eb"), 0.0)
    ts(col("pw", 0), a("pi"), 15, A.bitwise_and)
    ts(col("pw", 1), a("pi"), 1, A.bitwise_and)
    ms(a("keep"), 1.0)
    cp(a("pf", 0, 2), a("pw", 0, 2))
    ts(a("eb", 3, 515, 4), a("d128"), 0.0, A.is_equal)
    ms(a("keep", 0, C, 16), 0.0)
    ts(a("m16"), a("k16", 0, 16), 1.0 / 16, A.mult, Q16, A.is_equal)
    ts(a("qo"), a("k16"), 0.0, A.mult, Q16, A.add)
    lin(EVEN, ODD, -1.0, 1.0)
    lin(CQ, Q16, -STEP, 15 * STEP)
    lin(a("nid"), a("k16"), bias=Q16)
    act(a("m01"), ind(a("m16"), a("qo")), AF.Copy)
    lin(BQ, Q16, STEP - 1, 15 - 15 * STEP)
    lin(C2, Q16, -2 * STEP, 30 * STEP)
    lin(a("kl"), a("m01"), -BIG, STEP)
    lin(a("mbig"), a("m01"), 2 * BIG, -BIG)
    lin(C3, Q16, -STEP, 15 * STEP + 3.0 * LV)
    lin(col("rs", 0), Q16, 0.0)
    lin(a("base"), a("k16"), bias=BQ)
    lin(a("cc", 0, 40, 2), a("k16"), 0.0, -BIG)

    la = a("lf")
    quant("qe", "se", 0, 128, a("eb", 3, 515))
    for k in range(4):
        quant("qx", "sx", B * k, B * k + 128, a("ring", X0 + LV * k, X0 + LV * k + 512))
        if k == 0:
            send("arr0", "lq", a("qx", 0, B), 0, B, 0, 2)
            iota(a("pof"), [[1, 2], [16, 8]])
            iota(a("tab"), [[256, 16]])
        if k < 3:
            quant("qe", "se", 128 * k + 128, 128 * k + 256, a("eb", 2 - k, 514 - k))
    send("arr0", "ls", a("sx", 0, 4 * B), 0, 4 * B, 1, 2)
    came = send("arr0", "lq", a("qx", B, 4 * B), B, 4 * B)
    load("y", "dw", a("qw"), T.wc[:], after=[came], codes=True)
    load("y", "dw", a("sw"), T.ws[:])
    load("y", "dv", a("vb"), T.v[:])
    iota(a("ob"), [[0, 512]], 1)
    keep_where(a("ob"), [[-16, 8], [0, 64]], 0, 1)
    keep_where(a("ob"), [[16, 8], [0, 64]], 15, -1)
    for lo, n, planes in TILES:
        iota(a("ct", lo + 4 * 16 * planes[3], lo + 4 * n), [[0, 4 * n - 64 * planes[3]]])

    def last_table():
        iota(a("tabl"), [[1, 3], [0, 80]], -1)
        for lag in (-1, 0, 1):
            for d in range(3):
                up, down = 80 * (lag + 1) + 20 * d + 7, 80 * (lag + 1) + 20 * d + 20
                iota(a("tabl", up, up + 11, 5), [[0, 3]], lag + 1)
                iota(a("tabl", down, down + 11, 5), [[0, 3]], lag - 1)

    ts(a("ds"), a("li", 40, 60), float(LV), A.mult)
    ts(a("a4"), a("li", 0, 20), 4.0, A.mult)
    cp(a("au"), a("li", 0, 20))
    cp(la, a("li", 0, 20))
    tt(a("dl"), a("ds"), a("a4"), A.add)
    ts(a("d5"), a("ds"), 1.0 / 256, A.mult)
    cp(a("po"), a("pof"))
    for t in range(4):
        ts(a("oo", 20 * t, 20 * t + 20), a("dl"), float(t), A.add)
    lin(a("pb", 0, 20), la, ODD)
    lin(a("pb", 20, 40), la, EVEN)
    lin(a("pa", 40, 60), a("nid"), EVEN)
    lin(a("pa", 60, 80), a("nid"), ODD)
    for j in range(4):
        lin(a("a44", 20 * j, 20 * j + 20), la, 4.0, (CQ, C2)[j // 2])
    scatter(a("cb"), a("au"), a("i1"))
    ts(a("ph", 0, 20), a("li", 60, 80), float(B), A.mult)
    ts(a("kk"), a("keep"), 3 * BIG, A.mult, -3 * BIG, A.add)
    pull(a("ocl"), a("kl"), a("cb"))
    quant("qu", "su", 0, 128, a("ub"))
    ts(a("pa", 0, 20), ends("ocl"), CQ, A.subtract, EVEN, A.mult)
    ts(a("pa", 20, 40), ends("ocl"), CQ, A.subtract, ODD, A.mult)
    tt(a("pc", 40, 80), a("pa", 40, 80), a("pb"), A.add)
    tt(a("pc", 0, 40), a("pa", 0, 40), a("pb"), A.add)
    add("v", lambda: V.tensor_copy(T.qup[:, 0:256].bitcast(dt.uint32),
                                   T.qu[:, 0:128].bitcast(dt.uint32).indirect(T.po[:, 0:16])),
        [a("qu"), a("po")], [a("qup")])
    cp(a("pu"), a("pc"))
    tt(a("ph", 20, 40), a("ph", 0, 20), a("li", 20, 40), A.add)
    for f, scale, bias in ((F0, 1 / 16, -1 / 16), (F1, 1 / 64, -1 / 64), (F2, -1 / 8, 1 / 16), (F3, 3 / 64, 1 / 64),
                           (F4, -1 / 256, 1 / 256), (F5, 9 / 256, -281 / 256), (F6, 75.0, 81.0),
                           (SG0, -2.0 * LV, float(LV)), (SG1, 2.0 * LV, -float(LV))):
        lin(f, ODD, scale, bias)
    lin(w0(1), a("a4"), F1)
    lin(F7, CQ, F5, F6)

    def delays_out():
        act(a("dbb"), ind(a("tab"), a("d5")), AF.Copy)

    def own(r, t, q):
        src = ind(a("ring", (2 - r) * LV, (6 - r) * LV), a("oo", 20 * t, 20 * t + 20))
        scaled(q, a("ownh", C * t, C * t + C), src, 0.5)

    def partner_pick(r):
        act(a("mpp"), ind(a("dbb"), a("pu", 20 * (r % 2), 20 * (r % 2) + 20)), AF.Copy)

    def partner_scan():
        pull(a("spp"), a("kl"), a("mpp"))

    def far(r, order, lo, hi):
        for t in order:
            win = a("bord", 6 * B * t + (2 - r) * B, 6 * B * t + (6 - r) * B)
            tt(a("z", 4 * lo + t, 4 * hi, 4), ind(win, a("fo", lo // 16, hi // 16)), a("ownh", C * t + lo, C * t + hi), A.add)

    def packz(lo, hi):
        quant("qz", "sz", lo, hi, a("z", 4 * lo, 4 * hi))

    place = {}
    for lo, n, planes in TILES:
        for t, k in enumerate(planes):
            place[k] = lo + t

    def plane(k):
        return a("ct", place[k], place[k] + 4 * (16 * k if k else C) - 3, 4)

    def score(k):
        return col("oh", 16 * k + 15)

    def compare(ks):
        for k in ks:
            if k not in SP:
                ts(plane(k), bank(0, 0, 16 * k), score(k), A.is_lt)

    def pack(m):
        lo, n, _p = TILES[m]
        quant("qc", "sc", lo // 4, lo // 4 + n, a("ct", lo, lo + 4 * n))

    def count(m, start, stop):
        lo, n, planes = TILES[m]
        mm(3, "qe", "se", 512, "qc", "sc", lo // 4, lo // 4 + n, start, stop)

    WS = 16 * max(VS)

    def rows(k):
        end = WS * (k - VS[0] + 1)
        scan(a("rsc", end - 16 * k, end), plane(k), plane(k), 0.0, A.add, A.max)

    delays_out()
    lin(w0(0), a("dl"), F0, F7)
    for t in range(4):
        own(0, t, "s")
    for h in range(2):
        mm(3 + h, "qe", "se", 0, "lq", "ls", 2 * B * h, 2 * B * h + 2 * B)
        scaled("vs"[h], a("bord", 2 * B * (h + 1), 2 * B * (h + 2)), bank(3 + h, 0, 2 * B), 0.5)
    cp(a("fo"), a("ph", 20, 40))
    for b in range(1, 4):
        mm(4 + b, "qe", "se", 128 * b, "lq", "ls", 0, 4 * B)
    for b in range(1, 4):
        scaled("s", a("bord", 6 * B * b + 2 * B, 6 * B * (b + 1)), bank(4 + b, 0, 4 * B), 0.5)
    add("s", lambda: S.activation(T.sup[:, 0:256], T.su[:, 0:128].indirect(T.po[:, 0:16]), AF.Copy),
        [a("su"), a("po")], [a("sup")])

    for r in range(R - 1):
        at, land = (1 - r) * LV, 4 * B + C * r
        if r == 1:
            delays_out()
        partner_pick(r)
        if r == 1:
            lin(w0(2), a("dn", 1, 40, 2), F2)
        far(r, (0, 1, 2), 0, C)
        far(r, (3,), 0, C // 2)
        far(r, (3,), C // 2, C)
        packz(0, C // 2)
        packz(C // 2, C)
        mm(0, "qup", "sup", 0, "qz", "sz", 0, C)
        for b in range(4):
            mm(4 + b, "qw", "sw", 128 * b, "qz", "sz", 0, C)
        mm(1, "qup", "sup", 0, "qz", "sz", 0, C)
        mm(2, "qup", "sup", 128, "qz", "sz", 0, C)
        for b in range(4):
            scaled("s", a("ring", at + b, at + LV, 4), bank(4 + b), 0.03125)
        partner_scan()
        if r == 0:
            quant("qe", "se", 512, 640, a("ob"))
        else:
            quant("qv", "sv", 0, 128, a("vb"))
        tt(a("sm"), ends("spp"), a("ds"), A.add)
        tt(a("mp", CUT, C), bank(0, CUT, C), a("mbig", CUT, C), A.min)
        tt(a("mp", 0, CUT), bank(0, 0, CUT), a("mbig", 0, CUT), A.min)
        pull(a("oh", CUT, C), a("kk", CUT, C), a("mp", CUT, C))
        pull(a("oh", 0, CUT), a("kk", 0, CUT), a("mp", 0, CUT))
        for j in range(len(SP) + 1):
            if j < len(SP):
                k = SP[j]
                act(a("sgn2", C * k, C * k + 16 * k), bank(1, 0, 16 * k), AF.Sign, bias=score(k), scale=-1.0)
            if j > 0:
                k = SP[j - 1]
                act(plane(k), a("sgn2", C * k, C * k + 16 * k), AF.Relu, acc=col("rs", k))
        compare((19, 18, 17, 16, 15, 14, 13))
        tt(plane(0), a("oh"), bank(0), A.is_ge)
        quant("qs", "ss", C * r, C * r + C, a("ring", at, at + LV))
        send("arr%d" % (r + 1), "lq", a("qs", C * r, C * r + C), land, land + C)
        send("arr%d" % (r + 1), "ls", a("ss", C * r, C * r + C), land, land + C)
        if r == 0:
            last_table()
        compare((12, 11, 10, 9))
        scan(a("seg"), a("keep"), plane(0), 0.0, A.mult, A.add)
        pack(2)
        compare((8, 7, 6, 5))
        compare((4, 3, 2, 1))
        pack(0)
        pack(3)
        pack(4)
        pack(1)
        for j, m in enumerate((0, 2, 3, 4, 1)):
            count(m, j == 0, j == 4)
        for k in range(19, 0, -1):
            if k not in SP and k not in VS:
                act(a("sgn2", C * k, C * k + 16 * k), plane(k), AF.Identity, acc=col("rs", k))
        act(a("sgn"), bank(2), AF.Sign)
        lin(a("ml"), ind(a("sgn"), a("pu", 40 + 20 * r, 60 + 20 * r)), (SG0, SG1)[r])
        for b in range(4):
            mm(4 + b, "qe", "se", 128 * b, "lq", "ls", land, land + C)
        for b in range(4):
            scaled("s", a("hp", C * b, C * b + C), bank(4 + b), 0.5)
        old, new = (a("dl"), a("dn", 1, 40, 2))[r], a("dn", 40 * r + 1, 40 * r + 40, 2)
        shift = (CQ, C2)[r]
        for k in VS:
            rows(k)
        tt(a("t1"), a("base"), ends("seg"), A.subtract)
        cp(a("rs", VS[0], VS[-1] + 1), a("rsc", WS - 1, WS * len(VS), WS))
        pull(a("o2"), a("kl"), bank(3))
        tt(a("rp"), a("t1"), a("rs"), A.subtract)
        ts(a("hlo", 20, 40), a("sm"), C3, A.subtract, 0.0, A.max)
        ts(a("hlo", 0, 20), a("sm"), CQ, A.subtract, 3.0 * LV, A.min)
        tt(a("rk"), ends("o2"), a("rp"), A.add)
        tt(a("cc", 1, 80, 2), a("hlo"), a("a44", 40 * r, 40 * r + 40), A.add)
        cp(a("ru"), a("rk"))
        if r == 1:
            tt(w1(0), w0(0), w0(1), A.add)
        scatter(a("ee"), a("ru"), a("i1"))
        pull(a("sl"), a("kl"), a("ml"))
        pull(a("oe"), a("kl", 0, B), a("ee", 0, B))
        tt(a("cc", 40, 80, 2), old, ends("sl"), A.add)
        if r == 1:
            tt(w1(1), w1(0), w0(2), A.add)
        ts(a("go", 8 * r, 8 * r + 6), a("oe", 15, B, 16), CQ, A.subtract)
        send("lst%d" % (r + 1), "gin", a("go", 8 * r, 8 * r + 6), 8 * r, 8 * r + 6)
        scan(a("dn", 40 * r, 40 * r + 40), a("cc", 0, 40), a("cc", 40, 80), 0.0, A.min, A.max)

        def offs(t):
            ts(a("oo", 20 * t, 20 * t + 20), new, shift, A.subtract, float(t), A.add)

        def pick(t, q):
            lo = 6 * B * t + (1 - r) * B
            scaled(q, a("bord", lo, lo + B), ind(a("hp", C * t, C * t + C), a("gin", 8 * r, 8 * r + 6)), 1.0)

        offs(1)
        offs(0)
        offs(2)
        own(r + 1, 0, "v")
        own(r + 1, 1, "s")
        tt(a("ds"), new, a("a44", 40 * r, 40 * r + 20), A.subtract)
        offs(3)
        pick(0, "v")
        ts(a("d5"), a("ds"), 1.0 / 256, A.mult)
        pick(1, "s")
        own(r + 1, 2, "s")
        pick(2, "s")
        own(r + 1, 3, "s")
        pick(3, "s")

    banks = ((4, 5, 6, 7, 2, 5), (0, 1, 3, 4, 2, 6))
    piece = ((0, HC), (HC, C))

    def layer(h):
        lo, hi = piece[h]
        mm(banks[h][4], "qup", "sup", 128, "qz", "sz", lo, hi)
        for b in (1, 0, 3, 2) if h else range(4):
            mm(banks[h][b], "qw", "sw", 128 * b, "qz", "sz", lo, hi)

    def evac(h, b, q):
        lo, hi = piece[h]
        scaled(q, a("hl", 4 * lo + b, 4 * hi, 4), bank(banks[h][b], 0, hi - lo), 0.03125)

    def signs(h):
        lo, hi = piece[h]
        act(a("sgn", lo, hi), bank(banks[h][4], 0, hi - lo), AF.Sign)

    def step(h, j):
        lo, hi = piece[h]
        if j == 0:
            pull(a("sf", lo, hi), a("kl", lo, hi), a("sgn", lo, hi))
        elif j == 1:
            tt(a("fi", lo // 16, hi // 16), a("sf", lo + 15, hi, 16), a("w1", 60 + lo // 16, 60 + hi // 16), A.add)
        elif j == 2:
            cp(a("fu", lo // 16, hi // 16), a("fi", lo // 16, hi // 16))
        else:
            scaled("sv"[h], a("lag", lo, hi), ind(a("tabl"), a("fu", lo // 16, hi // 16)), 1.0)

    def finish(h):
        lo, hi = piece[h]
        quant("qh", "sh", lo, hi, a("hl", 4 * lo, 4 * hi))
        mm(banks[h][5], "qv", "sv", 0, "qh", "sh", lo, hi)
        store("y", T.oc[:, 4 * lo:4 * hi], T.qh[:, lo:hi].bitcast(dt.uint8), a("qh", lo, hi))

    def result(h):
        lo, hi = piece[h]
        act(a("ysb", lo, hi), bank(banks[h][5], 0, hi - lo), AF.Copy)
        if h == 0:
            step(0, 3)
        store("s", T.y[:, lo:hi], T.ysb[:, lo:hi], a("ysb", lo, hi))

    delays_out()
    partner_pick(2)
    for t, h in ((0, 0), (1, 0), (0, 1), (2, 0), (1, 1), (3, 0)):
        far(2, (t,), *piece[h])
    ts(w0(3), a("dn", 41, 80, 2), F3, A.mult)
    packz(0, HC)
    layer(0)
    signs(0)
    for b in range(3):
        evac(0, b, "s")
    far(2, (2,), HC, C)
    tt(w1(2), w1(1), w0(3), A.add)
    far(2, (3,), HC, C)
    partner_scan()
    packz(HC, C)
    layer(1)
    ts(w0(4), ends("spp"), F4, A.mult)
    evac(0, 3, "v")
    step(0, 0)
    tt(w1(3), w1(2), w0(4), A.add)
    finish(0)
    signs(1)
    evac(1, 0, "s")
    evac(1, 1, "v")
    step(0, 1)
    evac(1, 2, "s")
    evac(1, 3, "v")
    step(0, 2)
    step(1, 0)
    finish(1)
    for k in range(4):
        store("y", T.osc[4 * k:4 * k + 4, :], T.sh[32 * k:32 * k + 4, :], a("sh"))
    step(1, 1)
    result(0)
    step(1, 2)
    result(1)
    step(1, 3)
    store("y", T.ol[:], T.lag[0:128:16, 0:C], a("lag"))
    total = schedule(ops, queues, T)
    Y.wait_ge(T.sem.dout, total["dout"])
    g.wait_ge(T.sem.snt, total["snt"])
